import numpy as np, ml_dtypes
CORES = [9,25,41,57]
N = 4
import mx_ref
BF = ml_dtypes.bfloat16
def gcols(t, e):
    v = np.concatenate([t.reshape(8, 16, -1, 4), np.zeros((8, 16, 1, 4), BF)], axis=2)
    return np.ascontiguousarray(np.stack([v[g][:, e[g]] for g in range(8)])).reshape(128, -1)
def tile(rs):
    return np.stack(rs, axis=2).reshape(128, -1).astype(BF)
def cut(t, i, w=512):
    return t[:, w * i:w * i + w]
def pick(q, e):
    c = np.concatenate([q[0].reshape(128, -1, 4), np.zeros((128, 1, 4), np.uint8)], axis=1); s = np.concatenate([q[1], np.ones((16, 1), np.uint8)], axis=1)
    return (np.ascontiguousarray(c[:, e].reshape(128, -1)), np.ascontiguousarray(s[:, e]))
def join(*qs):
    return (np.concatenate([q[0] for q in qs], axis=1), np.concatenate([q[1] for q in qs], axis=1))
def put(q, e, v):
    c, s = q[0].reshape(128, -1, 4).copy(), q[1].copy(); c[:, e] = v[0].reshape(128, -1, 4); s[:, e] = v[1]
    return (c.reshape(128, -1), s)
def pk(c, s):
    return (np.ascontiguousarray(c), mx_ref.live(s))
def emit(q):
    return q[0], q[1]
def packed(v, rng):
    q = [mx_ref.quantize(np.ascontiguousarray(v[r])) for r in range(N)]
    return np.stack([a for a, b in q]), np.stack([mx_ref.plane(b, rng) for a, b in q])
def values_of_codes():
    e, c = np.zeros((128, 128, 4), np.float32), np.zeros((128, 2, 4), np.uint8)
    e[np.arange(128), np.arange(128), 0] = 1
    c[:127, :, 0] = np.arange(256).reshape(2, 128).T[:127]
    return mx_ref.matmul(mx_ref.quantize(e.reshape(128, 512).astype(BF)), (c.reshape(128, 8), np.full((16, 2), 127, np.uint8))).T.reshape(-1).astype(np.float64)
CODE_VALUE, SCALE_VALUE = values_of_codes(), 2.0 ** (np.arange(256) - 127.0)
def decode(q):
    return (CODE_VALUE[q[0]].reshape(16, 8, -1, 4) * SCALE_VALUE[q[1]][:, None, :, None] + 0.0).reshape(128, -1).astype(np.float32)
def f(rng, *shape):
    return mx_ref.flush((rng.standard_normal(shape, dtype=np.float32) * np.exp2(rng.integers(-2, 3, shape[:-1] + (1,)))).astype(BF))
def wide(rng, *shape, cols=0):
    v = rng.standard_normal(shape, dtype=np.float32) * np.exp2(rng.integers(-12, 13, shape)).astype(np.float32)
    if cols: v *= np.repeat(np.exp2(rng.integers(-cols, cols + 1, shape[:-2] + (1, shape[-1] // 4))) * (rng.random(shape[:-2] + (1, shape[-1] // 4)) > 0.0625), 4, axis=-1).astype(np.float32)
    return mx_ref.flush(v.astype(BF))
C, L, CAP, R = 512, 6, 144, 2
def windows(p):
    s = np.concatenate([p + np.float32(0.0), np.full((8, L - 1), np.inf, np.float32)], axis=1)
    return np.arange(C) + np.argmin(np.stack([s[:, i:i + C] for i in range(L)]), axis=0)
def coarse(v):
    v = np.array(v.astype(np.float32))
    v[np.abs(v) < np.float32(2.0 ** -16)] = 0
    return v.astype(BF)
def numbers_of(rng):
    return {"x": coarse(f(rng, N, 128, 4 * C)), "u": np.array(f(rng, N, 128, 512)), "v": np.array(f(rng, N, 128, 512))}
def sealed(rng, w):
    c, p = packed(np.ascontiguousarray(w).reshape(N, 128, 2048), rng)
    return {"wc": c, "ws": p}
def weights(rng, still=None):
    w = coarse(f(rng, N, 128, 2048)).reshape(N, 128, 4, 128, 4)
    if still is not None: w[:, :, :, np.flatnonzero(still)] = 0
    return sealed(rng, w)
def signs(rng):
    return np.stack([rng.permutation(8) % 2 * 2.0 - 1.0 for r in range(N)])
def plant(rng, s, z=np.ones(N)):
    d = numbers_of(rng)
    x = d["x"].astype(np.float32).reshape(N, 8, 16, C, 4)
    u = d["u"].reshape(N, 128, 128, 4)
    z = z.astype(np.float32).astype(BF)
    x[:, :, 0] = 0
    x[:, :, 0, :, 0] = signs(rng)[:, :, None]
    k = 8 + 2 * R
    x[:, :, k:] = rng.integers(4, 8, (N, 8, 16 - k, C, 4)) * rng.choice([-1.0, 1.0], (N, 8, 16 - k, C, 4)) * 2.0 ** -20
    for t in range(R):
        g = ((s[:, :, t, :, None] >> np.arange(8)) & 1) * np.exp2(np.arange(8) - 23.0)
        x[:, :, 8 + 2 * t] = g[..., :4]
        x[:, :, 9 + 2 * t] = g[..., 4:]
        u[:, :, t::16] = 0
        for h in range(0, 128, 16):
            u[:, h, h + t, 0] = z
            u[:, h + 8 + 2 * t:h + 10 + 2 * t, h + t] = z[:, None, None]
    i = np.arange(128) % 16
    return {"x": x.reshape(N, 128, 4 * C).astype(BF), "u": u.reshape(N, 128, 512), "v": d["v"], **weights(rng, (i == 0) | (i >= 8))}
def setup_inputs(rng):
    return {**numbers_of(rng), **weights(rng)}
def setup_inputs_ties(rng):
    d = numbers_of(rng)
    e = rng.permutation(N)
    x = d["x"].reshape(N, 8, 16, C, 4)
    for r in range(N):
        k = np.zeros(C, int) if r == e[0] else np.full(C, 2) if r == e[1] else rng.permutation(C) % 3
        a = x[r][:, :8, :3].copy()
        a[:, :, 2] = 0
        x[r][:, :8] = a[:, :, k]
    u = d["u"].reshape(N, 8, 16, 128, 4)
    for t in range(R): u[:, :, 8:, t::16] = 0
    return {"x": x.reshape(N, 128, 4 * C), "u": u.reshape(N, 128, 512), "v": d["v"], **weights(rng, np.arange(128) % 16 < 8)}
def setup_inputs_near(rng):
    j = np.arange(C)
    saw = 255 - (j + rng.integers(0, 12, (N, 8, R, 1))) % rng.integers(4, 13, (N, 8, R, 1))
    any8 = rng.integers(8, 16, (N, 8, R, C))
    b = np.stack([np.stack([rng.permutation(8) % 2 for t in range(R)], axis=1) for r in range(N)])
    return plant(rng, np.where(b[..., None] == 1, saw, any8), np.where(rng.permutation(N) < N // 2, 2.0 ** -30, 1.0))
def setup_inputs_slots(rng):
    j = np.arange(C)
    q = np.arange(C + 1)
    n = q + (C - 1 - q) // L + 1
    s = np.zeros((N, 8, R, C), int)
    for r in range(N):
        for t in range(R):
            want = rng.permutation(np.concatenate([[CAP - 1, CAP, CAP + 1, n[0], C], rng.integers(n[0], C + 1, 3)]))
            s[r, :, t] = np.where(j < np.searchsorted(n, want)[:, None], 0, 1 + (C - 1 - j) % L)
    return plant(rng, s)
def setup_inputs_huge(rng):
    d = numbers_of(rng)
    i = np.flatnonzero(np.arange(128) % 16 >= 14)
    x = 2.0 ** 30 * (0.7 + 0.3 * rng.random((N, 128, C, 4)))
    x[:, i] *= 0.25
    c = np.stack([rng.permutation(C) % 2 * 2.0 - 1.0 for r in range(N)])
    c[rng.permutation(N) < N // 2] = 1
    x *= c[:, None, :, None]
    u = d["u"].reshape(N, 128, 8, 16, 4)
    g = np.stack([signs(rng) for t in range(R)], axis=-1)
    a = 2.0 ** 30 * (0.7 + 0.3 * rng.random((N, 128, 8, R, 4))) * g[:, None, :, :, None]
    u[:, :, :, :R] = a.astype(np.float32).astype(BF)
    w = np.zeros((N, 128, 4, 128, 4), np.float32)
    for b in range(4): w[:, i, b, i, b] = 32
    return {"x": x.astype(np.float32).reshape(N, 128, 4 * C).astype(BF), "u": u.reshape(N, 128, 512), "v": d["v"], **sealed(rng, w.astype(BF))}
def setup_inputs_spread(rng):
    d = setup_inputs(rng)
    d["x"] = coarse(wide(rng, N, 128, 4 * C, cols=6))
    return d
def check_inputs(d):
    b = []
    for k in ("x", "u", "v"):
        a = np.abs(d[k].astype(np.float32))
        if not (np.isfinite(a).all() and ((a == 0) | (a >= 2.0 ** -30) & (a <= 2.0 ** 30)).all()): b.append("a value of " + k)
    return b
def reference(x, u, v, wc, ws):
    qu = [mx_ref.quantize(u[r]) for r in range(N)]
    lay = [pk(wc[r], ws[r]) for r in range(N)]
    now = [x[r] for r in range(N)]
    ol = np.zeros((N, 8, 2 * C), np.float32)
    for t in range(R):
        q = [mx_ref.quantize(now[r]) for r in range(N)]
        held = decode(join(*q))
        numbers, far = [], []
        for r in range(N):
            m = windows(mx_ref.matmul(qu[r], q[r])[t::16])
            hit = np.zeros((8, C), bool)
            np.put_along_axis(hit, m, True, axis=1)
            upto = np.add.accumulate(hit, axis=1, dtype=np.int64)
            n = np.take_along_axis(upto, m, axis=1) - 1
            first = np.argsort(~hit, axis=1, kind="stable")[:, :CAP]
            e = np.where(np.arange(CAP) < upto[:, -1:], first, -1)
            p = mx_ref.quantize(gcols(cut(held, r, 4 * C).astype(BF), e))
            w = lay[(r + 1 + t) % N]
            far.append(mx_ref.quantize(tile([mx_ref.matmul(pick(w, np.arange(128 * b, 128 * b + 128)), p) * np.float32(0.03125) for b in range(4)])))
            numbers.append(n)
            ol[r] = np.concatenate([m, n], axis=1)
        came = decode(join(*far)).astype(BF)
        for r in range(N):
            add = gcols(cut(came, r, 4 * CAP), np.where(numbers[r] < CAP, numbers[r], -1))
            now[r] = np.ascontiguousarray((cut(held, r, 4 * C) + add.astype(np.float32)).astype(BF))
    y = np.zeros((N, 128, C), np.float32)
    oc, osc = np.zeros((N, 128, 4 * C), np.uint8), np.zeros((N, 16, C), np.uint8)
    for r in range(N):
        last = mx_ref.quantize(now[r])
        y[r] = mx_ref.matmul(mx_ref.quantize(v[r]), last)
        oc[r], osc[r] = emit(last)
    return {"y": y, "ol": ol, "oc": oc, "osc": osc}

@@ -1,0 +1,389 @@
+from concourse.mybir import dt, AluOpType, AxisListType, ActivationFunctionType
+
+C, CAP, ROUNDS = 512, 144, 2
+BIG = 1.0e29
+FW = 528
+DW = 160
+AW = 4128
+F32, BF, U16, I32, X4, U8 = "float32", "bfloat16", "uint16", "int32", "float8_e4m3fn_x4", "uint8"
+
+
+def _sb(n, d):
+    return ("sbuf", [128, n], d)
+
+
+SCRATCH = {
+    "xt": _sb(2048, BF), "ut": _sb(512, BF), "vt": _sb(512, BF), "t1": _sb(2048, BF), "t2": _sb(2048, BF),
+    "q0": _sb(512, X4), "s0": _sb(512, U8), "q1": _sb(512, X4), "s1": _sb(512, U8), "q2": _sb(512, X4), "s2": _sb(512, U8),
+    "qu": _sb(128, X4), "su": _sb(128, U8), "qv": _sb(128, X4), "sv": _sb(128, U8),
+    "wq": _sb(512, X4), "wp": _sb(512, U8),
+    "lq0": _sb(512, X4), "lp0": _sb(512, U8), "lq1": _sb(512, X4), "lp1": _sb(512, U8),
+    "eb": _sb(520, BF), "qe": _sb(512, X4), "se": _sb(512, U8),
+    "fp": _sb(4 * FW, BF), "dh": _sb(4 * DW, BF), "gb": _sb(2048, BF),
+    "pt": _sb(4 * CAP, BF), "qp": _sb(CAP, X4), "sp": _sb(CAP, U8),
+    "ht": _sb(4 * CAP, BF), "qh": _sb(CAP, X4), "sh": _sb(CAP, U8),
+    "ysb": _sb(512, F32), "olm": _sb(32, F32), "oln": _sb(32, F32),
+    "jj": _sb(128, F32), "pi": _sb(8, I32), "pf": _sb(8, F32), "pc": _sb(8, F32), "r16": _sb(CAP, F32), "pen": _sb(CAP, F32),
+    "vc": _sb(256, F32), "ct": _sb(16, F32), "d0": _sb(288, F32), "p4": _sb(4, F32), "ones": _sb(32, F32),
+    "m1": _sb(32, F32), "m2": _sb(32, F32), "msk": _sb(32, F32), "jc": _sb(32, F32),
+    "offg": _sb(12, U16), "offr": _sb(4, U16), "offf": _sb(2, U16),
+    "xs": _sb(576, F32), "zz": _sb(96, F32), "dd": _sb(96, F32),
+    "w2": _sb(72, F32), "w3": _sb(72, F32), "w4": _sb(72, F32), "w5": _sb(72, F32),
+    "nl": _sb(160, F32), "rr": _sb(160, F32), "ss": _sb(168, F32), "zf": _sb(32, F32), "loc": _sb(40, F32),
+    "mt": _sb(32, F32), "mtt": _sb(32, F32), "base": _sb(2, F32), "pp": _sb(16, F32), "nn": _sb(16, F32),
+    "qq": _sb(16, F32), "pl": _sb(16, F32), "offs": _sb(16, U16),
+    "a0": _sb(AW, F32), "a1": _sb(AW, F32), "e1": _sb(288, F32), "e2": _sb(CAP, F32), "offp": _sb(10, U16),
+    "c1": _sb(32, F32), "c2": _sb(32, F32), "ch": _sb(32, F32), "ln": _sb(32, F32), "nt": _sb(32, F32), "ntt": _sb(32, F32),
+    "nb": _sb(2, F32), "n2": _sb(64, F32), "n2t": _sb(64, F32), "offn": _sb(32, U16),
+    "m6": _sb(32, F32), "kf": _sb(160, F32), "ks": _sb(168, F32), "kd": _sb(32, F32),
+    "psf": ("psum", [128, 2048], F32), "psr": ("psum", [128, 2048], F32),
+}
+N_LOADS = 8
+SEMAPHORES = ["cv", "cs", "cp", "cg", "sent", "ap0", "aq0", "ap1", "aq1", "stored"] + ["d%d" % i for i in range(N_LOADS)]
+
+
+def rank_program(g, core, T, topo):
+    rank = T.rank_of(core)
+    if rank is None:
+        return
+    A, ACT = AluOpType, ActivationFunctionType
+    n_ranks = len(T.cores)
+    Q = {"v": g.vector, "s": g.scalar, "p": g.tensor, "g": g, "y": g.sync}
+    V, S = g.vector, g.scalar
+    count = {"cv": 0, "cs": 0, "cp": 0, "cg": 0, "stored": 0}
+    known = {e: {} for e in Q}
+    waited = {}
+    wrote, read = {}, {}
+    loads = []
+
+    def need(e, marks):
+        for m in sorted(marks, key=lambda k: -k[1]):
+            sem, val, clock = m[0], m[1], m[2]
+            if known[e].get(sem, 0) < val:
+                Q[e].wait_ge(T.sem[sem], val)
+                waited[sem] = max(waited.get(sem, 0), val)
+                known[e][sem] = val
+                for k, x in clock.items():
+                    if known[e].get(k, 0) < x:
+                        known[e][k] = x
+
+    def op(e, call, r=(), w=(), dma=False):
+        marks = []
+        for k in r:
+            if k in wrote:
+                marks.append(wrote[k])
+            if k[0] == "B":
+                marks += [m for m in read.get(k, []) if m[3] != e]
+        for k in w:
+            if k in wrote:
+                marks.append(wrote[k])
+            marks += read.get(k, [])
+        need(e, marks)
+        if dma and not w:
+            call().then_inc(T.sem.stored, 16)
+            count["stored"] += 16
+            return
+        if dma:
+            sem = "d%d" % len(loads)
+            call().then_inc(T.sem[sem], 16)
+            me = (sem, 16, dict(known[e]), "dma")
+            loads.append(me)
+        else:
+            sem = "c" + e
+            call().then_inc(T.sem[sem], 1)
+            count[sem] += 1
+            me = (sem, count[sem], dict(known[e]), e)
+        for k in r:
+            read.setdefault(k, []).append(me)
+        for k in w:
+            wrote[k] = me
+            read[k] = []
+
+    def tt(out, a, b, o, r, w):
+        op("v", lambda: V.tensor_tensor(out, a, b, o), r, w)
+
+    def ts(out, a, s1, o1, r, w, s2=None, o2=None):
+        if s2 is None:
+            op("v", lambda: V.tensor_scalar(out, a, s1, None, o1), r, w)
+        else:
+            op("v", lambda: V.tensor_scalar(out, a, s1, s2, o1, o2), r, w)
+
+    def cp(out, a, r, w):
+        op("v", lambda: V.tensor_copy(out, a), r, w)
+
+    def fill(out, c, w):
+        op("v", lambda: V.memset(out, c), (), w)
+
+    def tr(out, a, r, w):
+        op("v", lambda: V.transpose(out, a), r, w)
+
+    def total(out, a, r, w):
+        op("v", lambda: V.tensor_reduce(out, a, AxisListType.X, A.add), r, w)
+
+    def scan(out, a, b, init, o0, o1, r, w):
+        op("v", lambda: V.tensor_tensor_scan(out, a, b, init, o0, o1), r, w)
+
+    def act(out, a, r, w, scale=1.0):
+        op("s", lambda: S.activation(out, a, ACT.Copy, scale=scale), r, w)
+
+    def quant(q, s, a, r, w):
+        op("v", lambda: V.quantize_mx(q, s, a), r, w)
+
+    def mm(out, lq, ls, rq, rs, r, w):
+        op("p", lambda: g.tensor.matmul_mx(out, lq, ls, rq, rs, True, True), r, w)
+
+    def iota(out, pattern, base, cm, w, flag=True):
+        if flag:
+            op("g", lambda: g.iota(out, pattern, base, cm, allow_small_or_imprecise_dtypes=True), (), w)
+        else:
+            op("g", lambda: g.iota(out, pattern, base, cm), (), w)
+
+    def dma(e, out, a, r, w):
+        op(e, lambda: Q[e].dma_start(out, a), r, w, dma=True)
+
+    def bank(buf, b, n, first=0):
+        return buf[:, 512 * b + first:512 * b + first + n]
+
+    dma("s", T.wp[:], T.ws[:], (), ["wp"])
+    dma("y", T.xt[:, 0:1024], T.x[:, 0:1024], (), ["x0"])
+    dma("s", T.ut[:], T.u[:], (), ["ut"])
+    dma("s", T.xt[:, 1024:1536], T.x[:, 1024:1536], (), ["x1"])
+    dma("y", T.xt[:, 1536:2048], T.x[:, 1536:2048], (), ["x2"])
+    dma("y", T.wq[:].bitcast(dt.uint8), T.wc[:], (), ["wq"])
+    dma("y", T.vt[:], T.v[:], (), ["vt"])
+
+    sent = [0]
+
+    def send(dst_ap, src_ap, sem, t, key):
+        peer = T.cores[(rank - 1 - t) % n_ranks]
+        rid, pid, _ = topo.addr(peer)
+        need("g", [wrote[key]])
+        g.remote_dma(dst_ap, src_ap, T.sem[sem], T.sem.sent, pid, rid, topo.mask(core, peer))
+        sent[0] += len(topo.engines(core, peer))
+
+    for t in range(ROUNDS):
+        k = len(topo.engines(T.cores[(rank + 1 + t) % n_ranks], core))
+        wrote["lp%d" % t] = ("ap%d" % t, k, {}, "far")
+        wrote["lq%d" % t] = ("aq%d" % t, k, {}, "far")
+
+    iota(T.pi[:, 4:5], [[0, 1]], 0, 1, ["pi4"], flag=False)
+    iota(T.jj[:], [[1, 128]], 0, 0, ["jj"])
+    iota(T.r16[:], [[0, 9], [1, 16]], 0, 0, ["r16"])
+    iota(T.p4[:], [[16, 2], [0, 2]], 0, 0, ["p4"])
+    iota(T.ct[:], [[1, 16]], 1024, 16, ["ct"])
+    send(T.lp0[:], T.wp[:], "ap0", 0, "wp")
+    iota(T.d0[:], [[0, CAP], [1, 2]], 0, 0, ["d0"])
+    iota(T.vc[:], [[2, 16], [32, 16]], 1, 0, ["vc"])
+    send(T.lq0[:].bitcast(dt.uint8), T.wq[:].bitcast(dt.uint8), "aq0", 0, "wq")
+    send(T.lp1[:], T.wp[:], "ap1", 1, "wp")
+    send(T.lq1[:].bitcast(dt.uint8), T.wq[:].bitcast(dt.uint8), "aq1", 1, "wq")
+
+    fill(T.eb[:], 0.0, ["eb"])
+    fill(T.xs[:, 0:32], -BIG, ["xsl"])
+    fill(T.xs[:, 544:576], BIG, ["xsr"])
+    fill(T.ones[:], 1.0, ["ones"])
+    p = T.pi[:, 4:5]
+    ts(T.pi[:, 0:1], p, 15, A.bitwise_and, ["pi4"], ["pi0"])
+    ts(T.pi[:, 1:2], p, 16, A.bitwise_and, ["pi4"], ["pi1"])
+    ts(T.pi[:, 2:3], p, 1, A.bitwise_and, ["pi4"], ["pi2"])
+    ts(T.pi[:, 3:4], p, 1, A.logical_shift_right, ["pi4"], ["pi3"], 7, A.bitwise_and)
+    cp(T.pf[:, 0:5], T.pi[:, 0:5], ["pi0", "pi1", "pi2", "pi3", "pi4"], ["pf"])
+    piece, half, odd, pair, part = [T.pf[:, i:i + 1] for i in range(5)]
+    ts(T.eb[:, 3:515:4], T.jj[:], part, A.is_equal, ["jj", "pf", "eb"], ["eb"])
+    ts(T.pc[:, 0:1], piece, 32.0, A.mult, ["pf"], ["pc0"])
+    ts(T.pc[:, 1:2], piece, half, A.add, ["pf"], ["pc1"])
+    ts(T.pc[:, 2:3], odd, 32.0, A.mult, ["pf"], ["pc2"], half, A.add)
+    for b in range(4):
+        quant(T.qe[:, 128 * b:128 * b + 128], T.se[:, 128 * b:128 * b + 128], T.eb[:, 3 - b:515 - b], ["eb"], ["qe%d" % b])
+    for t in range(ROUNDS):
+        ts(T.offg[:, 6 * t:6 * t + 6], T.jj[:, 0:96:16], T.pc[:, 0:1], A.add, ["jj", "pc0"], ["offg%d" % t], float(t), A.add)
+    quant(T.qu[:], T.su[:], T.ut[:], ["ut"], ["qu"])
+    ts(T.m1[:], T.jj[:, 0:32], T.pc[:, 1:2], A.is_gt, ["jj", "pc1"], ["m1"])
+    ts(T.m2[:], T.jj[:, 0:32], half, A.subtract, ["jj", "pf"], ["m2"], 16.0, A.is_lt)
+
+    act(T.fp[:, C:4 * FW:FW], T.jj[:, 0:4], ["jj"], ["fz"], 0.0)
+    act(T.dh[:, CAP + 1:4 * DW:DW], T.jj[:, 0:4], ["jj"], ["dz"], 0.0)
+    act(T.dh[:, 0:4 * DW:DW], T.jj[:, 0:4], ["jj"], ["dz0"], 0.0)
+    act(T.ss[:, 4:5], T.jj[:, 0:1], ["jj"], ["ss0"], 0.0)
+    act(T.ks[:, 4:5], T.jj[:, 0:1], ["jj"], ["ks0"], 0.0)
+    act(T.loc[:, 0:1], T.jj[:, 0:1], ["jj"], ["loc0"], 0.0)
+    for win, ak in ((T.a0, "a0"), (T.a1, "a1")):
+        act(win[:, 0:CAP], T.r16[:], ["r16"], [ak + "l"], 0.0)
+        act(win[:, CAP:2 * CAP], T.r16[:], ["r16"], [ak], 0.0)
+
+    tiles = [T.xt, T.t1, T.t2]
+    codes = [(T.q0, T.s0), (T.q1, T.s1), (T.q2, T.s2)]
+    pieces = [[(0, 256), (256, 384), (384, 512)], [(0, 256), (256, 512)], [(0, 256), (256, 384), (384, 512)]]
+
+    def quant_piece(t, i, keys):
+        q, s = codes[t]
+        a, b = pieces[t][i]
+        quant(q[:, a:b], s[:, a:b], tiles[t][:, 4 * a:4 * b], keys, ["q%d%d" % (t, i)])
+        side = (T.qu[:], T.su[:], "qu") if t < ROUNDS else (T.qv[:], T.sv[:], "qv")
+        mm(bank(T.psr, i, b - a), side[0], side[1], q[:, a:b], s[:, a:b], [side[2], "q%d%d" % (t, i)], ["Br%d" % i])
+
+    def turn(t, i):
+        a, b = pieces[t][i]
+        tr(T.xs[:, 32 + a:32 + b], bank(T.psr, i, b - a), ["Br%d" % i], ["xs%d" % i])
+
+    quant_piece(0, 0, ["x0"])
+    tt(T.msk[:], T.m1[:], T.m2[:], A.mult, ["m1", "m2"], ["msk"])
+    ts(T.pen[:], T.r16[:], piece, A.is_le, ["r16", "pf"], ["pen"], 1024.0, A.mult)
+    ts(T.offr[:], T.p4[:], piece, A.add, ["p4", "pf"], ["offr"])
+    quant_piece(0, 1, ["x1"])
+    turn(0, 0)
+    quant_piece(0, 2, ["x2"])
+    turn(0, 1)
+    ts(T.offf[:], T.jj[:, 0:16:8], T.pc[:, 2:3], A.add, ["jj", "pc2", "pf"], ["offf"], pair, A.add)
+    ts(T.jc[:], T.jj[:, 0:32], T.pc[:, 0:1], A.add, ["jj", "pc0"], ["jc"])
+    turn(0, 2)
+    D = T.dd
+    W = [None, T.dd, T.w2, T.w3, T.w4, T.w5]
+    wk = [None, "dd", "w2", "w3", "w4", "w5"]
+
+    for t in range(ROUNDS):
+        last = t + 1 == ROUNDS
+        q, s = codes[t]
+        qk = ["q%d%d" % (t, i) for i in range(len(pieces[t]))]
+        for b in range(4):
+            e = slice(128 * b, 128 * b + 128)
+            mm(bank(T.psf, b, C), T.qe[:, e], T.se[:, e], q[:], s[:], qk + ["qe%d" % b], ["Bf%d" % b])
+        for b in range(4):
+            act(T.fp[:, FW * b:FW * b + C], bank(T.psf, b, C), ["Bf%d" % b], ["f%d" % b])
+        cp(T.zz[:], T.xs[:].indirect(T.offg[:, 6 * t:6 * t + 6]), ["xs0", "xs1", "xs2", "xsl", "xsr", "offg%d" % t], ["zz"])
+        tr(D[:], T.zz[:], ["zz"], ["dd"])
+
+        def flags(d):
+            tt(T.nl[:, d - 1:160:5], D[:, 32:64], W[d][:, 32 - d:64 - d], A.is_ge, ["dd", wk[d]], ["nl%d" % d])
+            tt(T.rr[:, d - 1:160:5], D[:, 32:64], W[d][:, 33:65], A.is_le, ["dd", wk[d]], ["rr%d" % d])
+
+        def above(d):
+            tt(T.kf[:, d - 1:160:5], W[d][:, 32:64], T.m6[:], A.is_gt, [wk[d], "m6"], ["kf%d" % d])
+
+        tt(T.w2[:, 27:68], D[:, 27:68], D[:, 28:69], A.min, ["dd"], ["w2"])
+        flags(1)
+        tt(T.w4[:, 27:66], T.w2[:, 27:66], T.w2[:, 29:68], A.min, ["w2"], ["w4"])
+        tt(T.w3[:, 27:67], T.w2[:, 27:67], D[:, 29:69], A.min, ["w2", "dd"], ["w3"])
+        flags(2)
+        tt(T.w5[:, 27:65], T.w4[:, 27:65], D[:, 31:69], A.min, ["w4", "dd"], ["w5"])
+        flags(3)
+        flags(4)
+        flags(5)
+        scan(T.ss[:, 5:165], T.nl[:], T.rr[:], 0.0, A.add, A.subtract,
+             ["nl%d" % d for d in range(1, 6)] + ["rr%d" % d for d in range(1, 6)], ["ss"])
+        tt(T.c1[:], D[:, 31:63], T.w5[:, 32:64], A.is_le, ["dd", "w5"], ["c1"])
+        tt(T.zf[:], T.ss[:, 9:165:5], T.ss[:, 4:160:5], A.is_gt, ["ss", "ss0"], ["zf"])
+        tt(T.c2[:], D[:, 37:69], T.w5[:, 32:64], A.is_lt, ["dd", "w5"], ["c2"])
+        scan(T.loc[:, 1:33], T.ones[:], T.zf[:], 0.0, A.add, A.subtract, ["ones", "zf"], ["loc"])
+        tt(T.ch[:], T.c1[:], T.c2[:], A.max, ["c1", "c2"], ["ch"])
+        ts(T.mt[:], T.msk[:], T.loc[:, 32:33], A.mult, ["msk", "loc"], ["mt"], 2.0, A.mult)
+        tt(T.nn[:], T.loc[:, 0:32:2], T.loc[:, 2:34:2], A.is_equal, ["loc", "loc0"], ["nn"])
+        tr(T.mtt[:], T.mt[:], ["mt"], ["mtt"])
+        tt(T.qq[:], T.nn[:], T.ct[:], A.mult, ["nn", "ct"], ["qq"])
+        tt(T.pp[:], T.loc[:, 0:32:2], T.loc[:, 1:33:2], A.add, ["loc", "loc0"], ["pp"])
+        total(T.base[:, 0:1], T.mtt[:], ["mtt"], ["base"])
+        tt(T.pl[:], T.pp[:], T.qq[:], A.add, ["pp", "qq"], ["pl"])
+        scan(T.ln[:], T.ch[:], T.ch[:], 0.0, A.add, A.max, ["ch"], ["ln"])
+        ts(T.offs[:], T.pl[:], T.base[:, 0:1], A.add, ["pl", "base"], ["offs"])
+        ts(T.nt[:], T.msk[:], T.ln[:, 31:32], A.mult, ["msk", "ln"], ["nt"])
+        win, ak = [T.a0, T.a1][t], "a%d" % t
+        cp(win[:].indirect(T.offs[:]), T.vc[:], ["offs", "vc"], [ak, ak + "l"])
+        tr(T.ntt[:], T.nt[:], ["nt"], ["ntt"])
+        scan(T.e1[:], T.d0[:], win[:, 0:288], 0.0, A.add, A.max, ["d0", ak], ["e1"])
+        total(T.nb[:, 0:1], T.ntt[:], ["ntt"], ["nb"])
+        scan(T.e2[:], T.pen[:], T.e1[:, 1:288:2], 0.0, A.add, A.min, ["pen", "e1"], ["e2"])
+        if last:
+            tt(T.m6[:], T.w5[:, 32:64], D[:, 37:69], A.min, ["w5", "dd"], ["m6"])
+        ts(T.offp[:, 0:9], T.e2[:, 15:CAP:16], -1.0, A.add, ["e2"], ["offp"], float(C), A.min)
+        if last:
+            above(1)
+        for b in range(4):
+            src = T.fp[:, FW * b:FW * b + C + 1].indirect(T.offp[:, 0:9])
+            (cp if b < 2 else act)(T.pt[:, b:4 * CAP:4], src, ["f%d" % b, "fz", "offp"], ["p%d" % b])
+        quant(T.qp[:], T.sp[:], T.pt[:], ["p0", "p1", "p2", "p3"], ["qp"])
+        lq, lp = [(T.lq0, T.lp0), (T.lq1, T.lp1)][t]
+        for b in (2, 0, 3, 1):
+            e = slice(128 * b, 128 * b + 128)
+            mm(bank(T.psr, b, CAP), lq[:, e], lp[:, e], T.qp[:], T.sp[:], ["qp", "lq%d" % t, "lp%d" % t], ["Br%d" % b])
+        ts(T.n2[:], T.ln[:].indirect(T.offr[:]), T.nb[:, 0:1], A.add, ["ln", "offr", "nb"], ["n2"], float(CAP + 1), A.min)
+        if last:
+            above(2)
+        tr(T.n2t[:], T.n2[:], ["n2"], ["n2t"])
+        for b in (2, 0, 3, 1):
+            if b < 2:
+                ts(T.ht[:, b:4 * CAP:4], bank(T.psr, b, CAP), 0.03125, A.mult, ["Br%d" % b], ["h%d" % b])
+            else:
+                act(T.ht[:, b:4 * CAP:4], bank(T.psr, b, CAP), ["Br%d" % b], ["h%d" % b], 0.03125)
+        quant(T.qh[:], T.sh[:], T.ht[:], ["h0", "h1", "h2", "h3"], ["qh"])
+        for b in (0, 2, 1, 3):
+            e = slice(128 * b, 128 * b + 128)
+            mm(bank(T.psr, b, CAP), T.qe[:, e], T.se[:, e], T.qh[:], T.sh[:], ["qh", "qe%d" % b], ["Br%d" % b])
+        cp(T.offn[:], T.n2t[:].indirect(T.offf[:]), ["n2t", "offf"], ["offn"])
+        if last:
+            above(3)
+
+        new = tiles[t + 1]
+
+        def held(b, by):
+            by(T.dh[:, DW * b + 1:DW * b + 1 + CAP], bank(T.psr, b, CAP), ["Br%d" % b], ["dh%d" % b])
+
+        def came(b, h):
+            return T.dh[:, DW * b:DW * b + CAP + 2].indirect(T.offn[:, 16 * h:16 * h + 16])
+
+        def fetch(b, h):
+            act(T.gb[:, 512 * b + 256 * h:512 * b + 256 * h + 256], came(b, h), ["dh%d" % b, "dz", "dz0", "offn"], ["g%d%d" % (b, h)])
+
+        def add(b, h, direct):
+            out = new[:, 1024 * h + b:1024 * h + 1024:4]
+            key = ["T%d%d" % (h, b)]
+            if direct:
+                tt(out, came(b, h), T.fp[:, FW * b + 256 * h:FW * b + 256 * h + 256], A.add, ["dh%d" % b, "dz", "dz0", "offn", "f%d" % b], key)
+            else:
+                tt(out, bank(T.psf, b, 256, 256 * h), T.gb[:, 512 * b + 256 * h:512 * b + 256 * h + 256], A.add, ["Bf%d" % b, "g%d%d" % (b, h)], key)
+
+        held(0, cp)
+        held(2, act)
+        held(1, act)
+        fetch(2, 0)
+        held(3, act)
+        fetch(3, 0)
+        fetch(1, 1)
+        fetch(2, 1)
+        fetch(3, 1)
+        if last:
+            above(4)
+        else:
+            quant(T.qv[:], T.sv[:], T.vt[:], ["vt"], ["qv"])
+        for b in range(4):
+            add(b, 0, b < 2)
+        quant_piece(t + 1, 0, ["T0%d" % b for b in range(4)])
+        if last:
+            dma("y", T.oc[:, 0:1024], T.q2[:, 0:256].bitcast(dt.uint8), ["q20"], [])
+            act(T.ysb[:, 0:256], bank(T.psr, 0, 256), ["Br0"], ["y0"])
+            dma("y", T.y[:, 0:256], T.ysb[:, 0:256], ["y0"], [])
+        for b in range(4):
+            add(b, 1, b < 1)
+        quant_piece(t + 1, 1, ["T1%d" % b for b in range(4)])
+        if not last:
+            turn(t + 1, 0)
+            turn(t + 1, 1)
+
+    quant_piece(ROUNDS, 2, ["T1%d" % b for b in range(4)])
+    act(T.ysb[:, 256:384], bank(T.psr, 1, 128), ["Br1"], ["y1"])
+    dma("y", T.oc[:, 1024:2048], T.q2[:, 256:512].bitcast(dt.uint8), ["q21", "q22"], [])
+    above(5)
+    ts(T.oln[:], T.ln[:], T.nb[:, 0:1], A.add, ["ln", "nb"], ["oln"], -1.0, A.add)
+    scan(T.ks[:, 5:165], T.kf[:], T.kf[:], 0.0, A.add, A.max, ["kf%d" % d for d in range(1, 6)], ["ks"])
+    act(T.ysb[:, 384:512], bank(T.psr, 2, 128), ["Br2"], ["y2"])
+    dma("s", T.y[:, 256:512], T.ysb[:, 256:512], ["y1", "y2"], [])
+    tt(T.kd[:], T.ks[:, 9:165:5], T.ks[:, 4:160:5], A.subtract, ["ks", "ks0"], ["kd"])
+    tt(T.olm[:], T.kd[:], T.jc[:], A.add, ["kd", "jc"], ["olm"])
+    for k in range(4):
+        dma("y" if k < 3 else "s", T.osc[4 * k:4 * k + 4, :], T.s2[32 * k:32 * k + 4, :], ["q20", "q21", "q22"], [])
+    dma("s", T.ol[:, C:2 * C], T.oln[:], ["oln"], [])
+    dma("y", T.ol[:, 0:C], T.olm[:], ["olm"], [])
+
+    g.wait_ge(T.sem.sent, sent[0])
+    for sem, val in count.items():
+        if waited.get(sem, 0) < val:
+            g.wait_ge(T.sem[sem], val)

@@ -4,42 +4,22 @@ C, CAP, ROUNDS = 512, 144, 2
 BIG = 1.0e29
 FW = 528
 DW = 160
-AW = 4128
 F32, BF, U16, I32, X4, U8 = "float32", "bfloat16", "uint16", "int32", "float8_e4m3fn_x4", "uint8"
-
-
-def _sb(n, d):
-    return ("sbuf", [128, n], d)
-
-
-SCRATCH = {
-    "xt": _sb(2048, BF), "ut": _sb(512, BF), "vt": _sb(512, BF), "t1": _sb(2048, BF), "t2": _sb(2048, BF),
-    "q0": _sb(512, X4), "s0": _sb(512, U8), "q1": _sb(512, X4), "s1": _sb(512, U8), "q2": _sb(512, X4), "s2": _sb(512, U8),
-    "qu": _sb(128, X4), "su": _sb(128, U8), "qv": _sb(128, X4), "sv": _sb(128, U8),
-    "wq": _sb(512, X4), "wp": _sb(512, U8),
-    "lq0": _sb(512, X4), "lp0": _sb(512, U8), "lq1": _sb(512, X4), "lp1": _sb(512, U8),
-    "eb": _sb(520, BF), "qe": _sb(512, X4), "se": _sb(512, U8),
-    "fp": _sb(4 * FW, BF), "dh": _sb(4 * DW, BF), "gb": _sb(2048, BF),
-    "pt": _sb(4 * CAP, BF), "qp": _sb(CAP, X4), "sp": _sb(CAP, U8),
-    "ht": _sb(4 * CAP, BF), "qh": _sb(CAP, X4), "sh": _sb(CAP, U8),
-    "ysb": _sb(512, F32), "olm": _sb(32, F32), "oln": _sb(32, F32),
-    "jj": _sb(128, F32), "pi": _sb(8, I32), "pf": _sb(8, F32), "pc": _sb(8, F32), "r16": _sb(CAP, F32), "pen": _sb(CAP, F32),
-    "vc": _sb(256, F32), "ct": _sb(16, F32), "d0": _sb(288, F32), "p4": _sb(4, F32), "ones": _sb(32, F32),
-    "m1": _sb(32, F32), "m2": _sb(32, F32), "msk": _sb(32, F32), "jc": _sb(32, F32),
-    "offg": _sb(12, U16), "offr": _sb(4, U16), "offf": _sb(2, U16),
-    "xs": _sb(576, F32), "zz": _sb(96, F32), "dd": _sb(96, F32),
-    "w2": _sb(72, F32), "w3": _sb(72, F32), "w4": _sb(72, F32), "w5": _sb(72, F32),
-    "nl": _sb(160, F32), "rr": _sb(160, F32), "ss": _sb(168, F32), "zf": _sb(32, F32), "loc": _sb(40, F32),
-    "mt": _sb(32, F32), "mtt": _sb(32, F32), "base": _sb(2, F32), "pp": _sb(16, F32), "nn": _sb(16, F32),
-    "qq": _sb(16, F32), "pl": _sb(16, F32), "offs": _sb(16, U16),
-    "a0": _sb(AW, F32), "a1": _sb(AW, F32), "e1": _sb(288, F32), "e2": _sb(CAP, F32), "offp": _sb(10, U16),
-    "c1": _sb(32, F32), "c2": _sb(32, F32), "ch": _sb(32, F32), "ln": _sb(32, F32), "nt": _sb(32, F32), "ntt": _sb(32, F32),
-    "nb": _sb(2, F32), "n2": _sb(64, F32), "n2t": _sb(64, F32), "offn": _sb(32, U16),
-    "m6": _sb(32, F32), "kf": _sb(160, F32), "ks": _sb(168, F32), "kd": _sb(32, F32),
-    "psf": ("psum", [128, 2048], F32), "psr": ("psum", [128, 2048], F32),
-}
-N_LOADS = 8
-SEMAPHORES = ["cv", "cs", "cp", "cg", "sent", "ap0", "aq0", "ap1", "aq1", "stored"] + ["d%d" % i for i in range(N_LOADS)]
+SCRATCH = {"psf": ("psum", [128, 2048], F32), "psr": ("psum", [128, 2048], F32)}
+for _d, _l in (
+    (BF, "xt 2048 ut 512 vt 512 t1 2048 t2 2048 eb 520 fp 2112 dh 640 gb 2048 pt 576 ht 576 ll 224 rr 208 hh 192"),
+    (X4, "q0 512 q1 512 q2 512 qu 128 qv 128 wq 512 lq0 512 lq1 512 qe 512 qp 144 qh 144"),
+    (U8, "s0 512 s1 512 s2 512 su 128 sv 128 wp 512 lp0 512 lp1 512 se 512 sp 144 sh 144"),
+    (I32, "pi 8"),
+    (U16, "offg 12 offr 4 offf 2 offs 16 offp 10 offn 32"),
+    (F32, "ysb 512 olm 32 oln 32 jj 128 pf 8 pc 8 r16 144 pen 144 vc 256 ct 16 d0 288 p4 4 m1 32 m2 32 msk 32 jc 32 "
+          "xs 576 zz 96 dd 96 w2 72 w3 72 w4 72 w5 72 loc 40 mt 32 mtt 32 base 2 pp 16 nn 16 qq 16 pl 16 "
+          "a0 4128 a1 4128 e1 288 e2 144 ch 32 ln 32 nt 32 ntt 32 nb 2 n2 64 n2t 64 m6 32 kf 160 ks 168 kd 32"),
+):
+    _w = _l.split()
+    for _i in range(0, len(_w), 2):
+        SCRATCH[_w[_i]] = ("sbuf", [128, int(_w[_i + 1])], _d)
+SEMAPHORES = ["cv", "cs", "cp", "cg", "sent", "ap0", "aq0", "ap1", "aq1", "stored"] + ["d%d" % i for i in range(10)]
 
 
 def rank_program(g, core, T, topo):
@@ -144,11 +124,11 @@ def rank_program(g, core, T, topo):
     def bank(buf, b, n, first=0):
         return buf[:, 512 * b + first:512 * b + first + n]
 
-    dma("s", T.wp[:], T.ws[:], (), ["wp"])
     dma("y", T.xt[:, 0:1024], T.x[:, 0:1024], (), ["x0"])
     dma("s", T.ut[:], T.u[:], (), ["ut"])
     dma("s", T.xt[:, 1024:1536], T.x[:, 1024:1536], (), ["x1"])
     dma("y", T.xt[:, 1536:2048], T.x[:, 1536:2048], (), ["x2"])
+    dma("s", T.wp[:], T.ws[:], (), ["wp"])
     dma("y", T.wq[:].bitcast(dt.uint8), T.wc[:], (), ["wq"])
     dma("y", T.vt[:], T.v[:], (), ["vt"])
 
@@ -171,9 +151,9 @@ def rank_program(g, core, T, topo):
     iota(T.r16[:], [[0, 9], [1, 16]], 0, 0, ["r16"])
     iota(T.p4[:], [[16, 2], [0, 2]], 0, 0, ["p4"])
     iota(T.ct[:], [[1, 16]], 1024, 16, ["ct"])
-    send(T.lp0[:], T.wp[:], "ap0", 0, "wp")
     iota(T.d0[:], [[0, CAP], [1, 2]], 0, 0, ["d0"])
     iota(T.vc[:], [[2, 16], [32, 16]], 1, 0, ["vc"])
+    send(T.lp0[:], T.wp[:], "ap0", 0, "wp")
     send(T.lq0[:].bitcast(dt.uint8), T.wq[:].bitcast(dt.uint8), "aq0", 0, "wq")
     send(T.lp1[:], T.wp[:], "ap1", 1, "wp")
     send(T.lq1[:].bitcast(dt.uint8), T.wq[:].bitcast(dt.uint8), "aq1", 1, "wq")
@@ -181,7 +161,7 @@ def rank_program(g, core, T, topo):
     fill(T.eb[:], 0.0, ["eb"])
     fill(T.xs[:, 0:32], -BIG, ["xsl"])
     fill(T.xs[:, 544:576], BIG, ["xsr"])
-    fill(T.ones[:], 1.0, ["ones"])
+    fill(T.rr[:, 6:198:6], 1.0, ["rr0"])
     p = T.pi[:, 4:5]
     ts(T.pi[:, 0:1], p, 15, A.bitwise_and, ["pi4"], ["pi0"])
     ts(T.pi[:, 1:2], p, 16, A.bitwise_and, ["pi4"], ["pi1"])
@@ -195,16 +175,12 @@ def rank_program(g, core, T, topo):
     ts(T.pc[:, 2:3], odd, 32.0, A.mult, ["pf"], ["pc2"], half, A.add)
     for b in range(4):
         quant(T.qe[:, 128 * b:128 * b + 128], T.se[:, 128 * b:128 * b + 128], T.eb[:, 3 - b:515 - b], ["eb"], ["qe%d" % b])
-    for t in range(ROUNDS):
-        ts(T.offg[:, 6 * t:6 * t + 6], T.jj[:, 0:96:16], T.pc[:, 0:1], A.add, ["jj", "pc0"], ["offg%d" % t], float(t), A.add)
     quant(T.qu[:], T.su[:], T.ut[:], ["ut"], ["qu"])
-    ts(T.m1[:], T.jj[:, 0:32], T.pc[:, 1:2], A.is_gt, ["jj", "pc1"], ["m1"])
-    ts(T.m2[:], T.jj[:, 0:32], half, A.subtract, ["jj", "pf"], ["m2"], 16.0, A.is_lt)
 
     act(T.fp[:, C:4 * FW:FW], T.jj[:, 0:4], ["jj"], ["fz"], 0.0)
     act(T.dh[:, CAP + 1:4 * DW:DW], T.jj[:, 0:4], ["jj"], ["dz"], 0.0)
     act(T.dh[:, 0:4 * DW:DW], T.jj[:, 0:4], ["jj"], ["dz0"], 0.0)
-    act(T.ss[:, 4:5], T.jj[:, 0:1], ["jj"], ["ss0"], 0.0)
+    act(T.ll[:, 0:192:6], T.jj[:, 0:32], ["jj"], ["ll0"], 0.0)
     act(T.ks[:, 4:5], T.jj[:, 0:1], ["jj"], ["ks0"], 0.0)
     act(T.loc[:, 0:1], T.jj[:, 0:1], ["jj"], ["loc0"], 0.0)
     for win, ak in ((T.a0, "a0"), (T.a1, "a1")):
@@ -213,30 +189,31 @@ def rank_program(g, core, T, topo):
 
     tiles = [T.xt, T.t1, T.t2]
     codes = [(T.q0, T.s0), (T.q1, T.s1), (T.q2, T.s2)]
-    pieces = [[(0, 256), (256, 384), (384, 512)], [(0, 256), (256, 512)], [(0, 256), (256, 384), (384, 512)]]
+    pieces = [(0, 256), (256, 384), (384, 512)]
 
     def quant_piece(t, i, keys):
         q, s = codes[t]
-        a, b = pieces[t][i]
+        a, b = pieces[i]
         quant(q[:, a:b], s[:, a:b], tiles[t][:, 4 * a:4 * b], keys, ["q%d%d" % (t, i)])
         side = (T.qu[:], T.su[:], "qu") if t < ROUNDS else (T.qv[:], T.sv[:], "qv")
         mm(bank(T.psr, i, b - a), side[0], side[1], q[:, a:b], s[:, a:b], [side[2], "q%d%d" % (t, i)], ["Br%d" % i])
 
-    def turn(t, i):
-        a, b = pieces[t][i]
+    def turn(i):
+        a, b = pieces[i]
         tr(T.xs[:, 32 + a:32 + b], bank(T.psr, i, b - a), ["Br%d" % i], ["xs%d" % i])
 
     quant_piece(0, 0, ["x0"])
-    tt(T.msk[:], T.m1[:], T.m2[:], A.mult, ["m1", "m2"], ["msk"])
-    ts(T.pen[:], T.r16[:], piece, A.is_le, ["r16", "pf"], ["pen"], 1024.0, A.mult)
-    ts(T.offr[:], T.p4[:], piece, A.add, ["p4", "pf"], ["offr"])
+    for t in range(ROUNDS):
+        ts(T.offg[:, 6 * t:6 * t + 6], T.jj[:, 0:96:16], T.pc[:, 0:1], A.add, ["jj", "pc0"], ["offg%d" % t], float(t), A.add)
+    ts(T.m1[:], T.jj[:, 0:32], T.pc[:, 1:2], A.is_gt, ["jj", "pc1"], ["m1"])
+    ts(T.m2[:], T.jj[:, 0:32], half, A.subtract, ["jj", "pf"], ["m2"], 16.0, A.is_lt)
     quant_piece(0, 1, ["x1"])
-    turn(0, 0)
+    turn(0)
     quant_piece(0, 2, ["x2"])
-    turn(0, 1)
-    ts(T.offf[:], T.jj[:, 0:16:8], T.pc[:, 2:3], A.add, ["jj", "pc2", "pf"], ["offf"], pair, A.add)
-    ts(T.jc[:], T.jj[:, 0:32], T.pc[:, 0:1], A.add, ["jj", "pc0"], ["jc"])
-    turn(0, 2)
+    turn(1)
+    tt(T.msk[:], T.m1[:], T.m2[:], A.mult, ["m1", "m2"], ["msk"])
+    ts(T.offr[:], T.p4[:], piece, A.add, ["p4", "pf"], ["offr"])
+    turn(2)
     D = T.dd
     W = [None, T.dd, T.w2, T.w3, T.w4, T.w5]
     wk = [None, "dd", "w2", "w3", "w4", "w5"]
@@ -244,18 +221,26 @@ def rank_program(g, core, T, topo):
     for t in range(ROUNDS):
         last = t + 1 == ROUNDS
         q, s = codes[t]
-        qk = ["q%d%d" % (t, i) for i in range(len(pieces[t]))]
+        qk = ["q%d%d" % (t, i) for i in range(3)]
         for b in range(4):
             e = slice(128 * b, 128 * b + 128)
             mm(bank(T.psf, b, C), T.qe[:, e], T.se[:, e], q[:], s[:], qk + ["qe%d" % b], ["Bf%d" % b])
         for b in range(4):
             act(T.fp[:, FW * b:FW * b + C], bank(T.psf, b, C), ["Bf%d" % b], ["f%d" % b])
+        if t == 0:
+            ts(T.offf[:], T.jj[:, 0:16:8], T.pc[:, 2:3], A.add, ["jj", "pc2", "pf"], ["offf"], pair, A.add)
         cp(T.zz[:], T.xs[:].indirect(T.offg[:, 6 * t:6 * t + 6]), ["xs0", "xs1", "xs2", "xsl", "xsr", "offg%d" % t], ["zz"])
+        if t == 0:
+            ts(T.jc[:], T.jj[:, 0:32], T.pc[:, 0:1], A.add, ["jj", "pc0"], ["jc"])
         tr(D[:], T.zz[:], ["zz"], ["dd"])
+        if t == 0:
+            ts(T.pen[:], T.r16[:], piece, A.is_le, ["r16", "pf"], ["pen"], 1024.0, A.mult)
 
         def flags(d):
-            tt(T.nl[:, d - 1:160:5], D[:, 32:64], W[d][:, 32 - d:64 - d], A.is_ge, ["dd", wk[d]], ["nl%d" % d])
-            tt(T.rr[:, d - 1:160:5], D[:, 32:64], W[d][:, 33:65], A.is_le, ["dd", wk[d]], ["rr%d" % d])
+            n = 37 if d == 5 else 32
+            o = 1 if d == 5 else 0
+            tt(T.ll[:, 6 - d:6 * n:6], D[:, 32:32 + n], W[d][:, 32 - d:32 + n - d], A.is_lt, ["dd", wk[d]], ["ll%d" % d])
+            tt(T.rr[:, 6 + d - 6 * o:198:6], D[:, 32 - o:64], W[d][:, 33 - o:65], A.is_le, ["dd", wk[d]], ["rr%d" % d])
 
         def above(d):
             tt(T.kf[:, d - 1:160:5], W[d][:, 32:64], T.m6[:], A.is_gt, [wk[d], "m6"], ["kf%d" % d])
@@ -269,13 +254,13 @@ def rank_program(g, core, T, topo):
         flags(3)
         flags(4)
         flags(5)
-        scan(T.ss[:, 5:165], T.nl[:], T.rr[:], 0.0, A.add, A.subtract,
-             ["nl%d" % d for d in range(1, 6)] + ["rr%d" % d for d in range(1, 6)], ["ss"])
-        tt(T.c1[:], D[:, 31:63], T.w5[:, 32:64], A.is_le, ["dd", "w5"], ["c1"])
-        tt(T.zf[:], T.ss[:, 9:165:5], T.ss[:, 4:160:5], A.is_gt, ["ss", "ss0"], ["zf"])
-        tt(T.c2[:], D[:, 37:69], T.w5[:, 32:64], A.is_lt, ["dd", "w5"], ["c2"])
-        scan(T.loc[:, 1:33], T.ones[:], T.zf[:], 0.0, A.add, A.subtract, ["ones", "zf"], ["loc"])
-        tt(T.ch[:], T.c1[:], T.c2[:], A.max, ["c1", "c2"], ["ch"])
+        if last:
+            tt(T.m6[:], T.w5[:, 32:64], D[:, 37:69], A.min, ["w5", "dd"], ["m6"])
+        scan(T.hh[:], T.ll[:, 0:192], T.rr[:, 6:198], 0.0, A.mult, A.max,
+             ["ll%d" % d for d in range(6)] + ["rr%d" % d for d in range(6)], ["hh"])
+        tt(T.ch[:], T.rr[:, 5:197:6], T.ll[:, 31:222:6], A.max, ["rr5", "ll5"], ["ch"])
+        scan(T.loc[:, 1:33], T.hh[:, 5:192:6], T.hh[:, 5:192:6], 0.0, A.add, A.max, ["hh"], ["loc"])
+        scan(T.ln[:], T.ch[:], T.ch[:], 0.0, A.add, A.max, ["ch"], ["ln"])
         ts(T.mt[:], T.msk[:], T.loc[:, 32:33], A.mult, ["msk", "loc"], ["mt"], 2.0, A.mult)
         tt(T.nn[:], T.loc[:, 0:32:2], T.loc[:, 2:34:2], A.is_equal, ["loc", "loc0"], ["nn"])
         tr(T.mtt[:], T.mt[:], ["mt"], ["mtt"])
@@ -283,23 +268,26 @@ def rank_program(g, core, T, topo):
         tt(T.pp[:], T.loc[:, 0:32:2], T.loc[:, 1:33:2], A.add, ["loc", "loc0"], ["pp"])
         total(T.base[:, 0:1], T.mtt[:], ["mtt"], ["base"])
         tt(T.pl[:], T.pp[:], T.qq[:], A.add, ["pp", "qq"], ["pl"])
-        scan(T.ln[:], T.ch[:], T.ch[:], 0.0, A.add, A.max, ["ch"], ["ln"])
-        ts(T.offs[:], T.pl[:], T.base[:, 0:1], A.add, ["pl", "base"], ["offs"])
         ts(T.nt[:], T.msk[:], T.ln[:, 31:32], A.mult, ["msk", "ln"], ["nt"])
+        ts(T.offs[:], T.pl[:], T.base[:, 0:1], A.add, ["pl", "base"], ["offs"])
+        tr(T.ntt[:], T.nt[:], ["nt"], ["ntt"])
         win, ak = [T.a0, T.a1][t], "a%d" % t
         cp(win[:].indirect(T.offs[:]), T.vc[:], ["offs", "vc"], [ak, ak + "l"])
-        tr(T.ntt[:], T.nt[:], ["nt"], ["ntt"])
-        scan(T.e1[:], T.d0[:], win[:, 0:288], 0.0, A.add, A.max, ["d0", ak], ["e1"])
         total(T.nb[:, 0:1], T.ntt[:], ["ntt"], ["nb"])
-        scan(T.e2[:], T.pen[:], T.e1[:, 1:288:2], 0.0, A.add, A.min, ["pen", "e1"], ["e2"])
-        if last:
-            tt(T.m6[:], T.w5[:, 32:64], D[:, 37:69], A.min, ["w5", "dd"], ["m6"])
-        ts(T.offp[:, 0:9], T.e2[:, 15:CAP:16], -1.0, A.add, ["e2"], ["offp"], float(C), A.min)
+        scan(T.e1[:], T.d0[:], win[:, 0:288], 0.0, A.add, A.max, ["d0", ak], ["e1"])
         if last:
             above(1)
+        scan(T.e2[:], T.pen[:], T.e1[:, 1:288:2], 0.0, A.add, A.min, ["pen", "e1"], ["e2"])
+        if last:
+            above(2)
+        ts(T.offp[:, 0:9], T.e2[:, 15:CAP:16], -1.0, A.add, ["e2"], ["offp"], float(C), A.min)
+        if last:
+            above(3)
         for b in range(4):
             src = T.fp[:, FW * b:FW * b + C + 1].indirect(T.offp[:, 0:9])
             (cp if b < 2 else act)(T.pt[:, b:4 * CAP:4], src, ["f%d" % b, "fz", "offp"], ["p%d" % b])
+        if last:
+            above(4)
         quant(T.qp[:], T.sp[:], T.pt[:], ["p0", "p1", "p2", "p3"], ["qp"])
         lq, lp = [(T.lq0, T.lp0), (T.lq1, T.lp1)][t]
         for b in (2, 0, 3, 1):
@@ -307,20 +295,25 @@ def rank_program(g, core, T, topo):
             mm(bank(T.psr, b, CAP), lq[:, e], lp[:, e], T.qp[:], T.sp[:], ["qp", "lq%d" % t, "lp%d" % t], ["Br%d" % b])
         ts(T.n2[:], T.ln[:].indirect(T.offr[:]), T.nb[:, 0:1], A.add, ["ln", "offr", "nb"], ["n2"], float(CAP + 1), A.min)
         if last:
-            above(2)
+            above(5)
         tr(T.n2t[:], T.n2[:], ["n2"], ["n2t"])
         for b in (2, 0, 3, 1):
             if b < 2:
                 ts(T.ht[:, b:4 * CAP:4], bank(T.psr, b, CAP), 0.03125, A.mult, ["Br%d" % b], ["h%d" % b])
             else:
                 act(T.ht[:, b:4 * CAP:4], bank(T.psr, b, CAP), ["Br%d" % b], ["h%d" % b], 0.03125)
+        if last:
+            ts(T.oln[:], T.ln[:], T.nb[:, 0:1], A.add, ["ln", "nb"], ["oln"], -1.0, A.add)
+            dma("y", T.ol[:, C:2 * C], T.oln[:], ["oln"], [])
         quant(T.qh[:], T.sh[:], T.ht[:], ["h0", "h1", "h2", "h3"], ["qh"])
         for b in (0, 2, 1, 3):
             e = slice(128 * b, 128 * b + 128)
             mm(bank(T.psr, b, CAP), T.qe[:, e], T.se[:, e], T.qh[:], T.sh[:], ["qh", "qe%d" % b], ["Br%d" % b])
         cp(T.offn[:], T.n2t[:].indirect(T.offf[:]), ["n2t", "offf"], ["offn"])
         if last:
-            above(3)
+            scan(T.ks[:, 5:165], T.kf[:], T.kf[:], 0.0, A.add, A.max, ["kf%d" % d for d in range(1, 6)], ["ks"])
+        else:
+            quant(T.qv[:], T.sv[:], T.vt[:], ["vt"], ["qv"])
 
         new = tiles[t + 1]
 
@@ -351,37 +344,34 @@ def rank_program(g, core, T, topo):
         fetch(2, 1)
         fetch(3, 1)
         if last:
-            above(4)
-        else:
-            quant(T.qv[:], T.sv[:], T.vt[:], ["vt"], ["qv"])
+            tt(T.kd[:], T.ks[:, 9:165:5], T.ks[:, 4:160:5], A.subtract, ["ks", "ks0"], ["kd"])
         for b in range(4):
             add(b, 0, b < 2)
+        add(0, 1, True)
         quant_piece(t + 1, 0, ["T0%d" % b for b in range(4)])
         if last:
             dma("y", T.oc[:, 0:1024], T.q2[:, 0:256].bitcast(dt.uint8), ["q20"], [])
             act(T.ysb[:, 0:256], bank(T.psr, 0, 256), ["Br0"], ["y0"])
+        for b in range(1, 4):
+            add(b, 1, False)
+        if last:
+            tt(T.olm[:], T.kd[:], T.jc[:], A.add, ["kd", "jc"], ["olm"])
             dma("y", T.y[:, 0:256], T.ysb[:, 0:256], ["y0"], [])
-        for b in range(4):
-            add(b, 1, b < 1)
+            dma("y", T.ol[:, 0:C], T.olm[:], ["olm"], [])
+        else:
+            turn(0)
         quant_piece(t + 1, 1, ["T1%d" % b for b in range(4)])
+        quant_piece(t + 1, 2, ["T1%d" % b for b in range(4)])
         if not last:
-            turn(t + 1, 0)
-            turn(t + 1, 1)
+            turn(1)
+            turn(2)
 
-    quant_piece(ROUNDS, 2, ["T1%d" % b for b in range(4)])
     act(T.ysb[:, 256:384], bank(T.psr, 1, 128), ["Br1"], ["y1"])
+    cp(T.ysb[:, 384:512], bank(T.psr, 2, 128), ["Br2"], ["y2"])
     dma("y", T.oc[:, 1024:2048], T.q2[:, 256:512].bitcast(dt.uint8), ["q21", "q22"], [])
-    above(5)
-    ts(T.oln[:], T.ln[:], T.nb[:, 0:1], A.add, ["ln", "nb"], ["oln"], -1.0, A.add)
-    scan(T.ks[:, 5:165], T.kf[:], T.kf[:], 0.0, A.add, A.max, ["kf%d" % d for d in range(1, 6)], ["ks"])
-    act(T.ysb[:, 384:512], bank(T.psr, 2, 128), ["Br2"], ["y2"])
     dma("s", T.y[:, 256:512], T.ysb[:, 256:512], ["y1", "y2"], [])
-    tt(T.kd[:], T.ks[:, 9:165:5], T.ks[:, 4:160:5], A.subtract, ["ks", "ks0"], ["kd"])
-    tt(T.olm[:], T.kd[:], T.jc[:], A.add, ["kd", "jc"], ["olm"])
     for k in range(4):
         dma("y" if k < 3 else "s", T.osc[4 * k:4 * k + 4, :], T.s2[32 * k:32 * k + 4, :], ["q20", "q21", "q22"], [])
-    dma("s", T.ol[:, C:2 * C], T.oln[:], ["oln"], [])
-    dma("y", T.ol[:, 0:C], T.olm[:], ["olm"], [])
 
     g.wait_ge(T.sem.sent, sent[0])
     for sem, val in count.items():

@@ -1,25 +1,31 @@
-from concourse.mybir import dt, AluOpType, AxisListType, ActivationFunctionType
+from concourse.mybir import dt, AluOpType, ActivationFunctionType
 
 C, CAP, ROUNDS = 512, 144, 2
 BIG = 1.0e29
-FW = 528
 DW = 160
+R0 = 224
 F32, BF, U16, I32, X4, U8 = "float32", "bfloat16", "uint16", "int32", "float8_e4m3fn_x4", "uint8"
 SCRATCH = {"psf": ("psum", [128, 2048], F32), "psr": ("psum", [128, 2048], F32)}
 for _d, _l in (
-    (BF, "xt 2048 ut 512 vt 512 t1 2048 t2 2048 eb 520 fp 2112 dh 640 gb 2048 pt 576 ht 576 ll 224 rr 208 hh 192"),
+    (BF, "xt 2048 ut 512 vt 512 t1 2048 t2 2048 eb 520 fp 2064 dh 640 gb 2048 pt 576 ht 576 lr 464 hh 208 "
+         "a0 4128 a1 4128 vc 256 d0 288 e1 288 e2 144 pen 144 mg 256 md 256 mk 256"),
     (X4, "q0 512 q1 512 q2 512 qu 128 qv 128 wq 512 lq0 512 lq1 512 qe 512 qp 144 qh 144"),
     (U8, "s0 512 s1 512 s2 512 su 128 sv 128 wp 512 lp0 512 lp1 512 se 512 sp 144 sh 144"),
-    (I32, "pi 8"),
-    (U16, "offg 12 offr 4 offf 2 offs 16 offp 10 offn 32"),
-    (F32, "ysb 512 olm 32 oln 32 jj 128 pf 8 pc 8 r16 144 pen 144 vc 256 ct 16 d0 288 p4 4 m1 32 m2 32 msk 32 jc 32 "
-          "xs 576 zz 96 dd 96 w2 72 w3 72 w4 72 w5 72 loc 40 mt 32 mtt 32 base 2 pp 16 nn 16 qq 16 pl 16 "
-          "a0 4128 a1 4128 e1 288 e2 144 ch 32 ln 32 nt 32 ntt 32 nb 2 n2 64 n2t 64 m6 32 kf 160 ks 168 kd 32"),
+    (I32, "pi 12"),
+    (U16, "offg 12 offr 4 offf 2 offs 16 offp 36 offn 32 offb 4 offm 16"),
+    (F32, "ysb 512 olm 32 oln 32 jj 128 pf 12 pc 16 r4 144 ct 16 p4 4 tab 544 xs 576 zz 96 dd 96 w2 72 w3 72 w4 72 w5 72 "
+          "pd 104 pm 64 pl 64 ch 32 base 2 nb 2 j0 16 j1 16 n2 64 n2t 64"),
 ):
     _w = _l.split()
     for _i in range(0, len(_w), 2):
         SCRATCH[_w[_i]] = ("sbuf", [128, int(_w[_i + 1])], _d)
 SEMAPHORES = ["cv", "cs", "cp", "cg", "sent", "ap0", "aq0", "ap1", "aq1", "stored"] + ["d%d" % i for i in range(10)]
+
+PLAN = [
+    "h0v h1s h2s h3s d00123 f20123 d3012 f1012 a20123 f13 a1012 f33 a13 q01 a33 q2 q3 t01 t2 t3",
+    "h0v h1s h2s h3s d0012 f20 d301 f10 f11 f12 a20 a10 a11 q0 c0 d21 f32 a32 a12 f22 y0s a22 q1 c1 f23 q2 c2 f13 d33 "
+    "y1s d03 a23 y2s a13 q3 c3 y3v",
+]
 
 
 def rank_program(g, core, T, topo):
@@ -50,8 +56,7 @@ def rank_program(g, core, T, topo):
     def op(e, call, r=(), w=(), dma=False):
         marks = []
         for k in r:
-            if k in wrote:
-                marks.append(wrote[k])
+            marks.append(wrote[k])
             if k[0] == "B":
                 marks += [m for m in read.get(k, []) if m[3] != e]
         for k in w:
@@ -97,14 +102,17 @@ def rank_program(g, core, T, topo):
     def tr(out, a, r, w):
         op("v", lambda: V.transpose(out, a), r, w)
 
-    def total(out, a, r, w):
-        op("v", lambda: V.tensor_reduce(out, a, AxisListType.X, A.add), r, w)
-
     def scan(out, a, b, init, o0, o1, r, w):
         op("v", lambda: V.tensor_tensor_scan(out, a, b, init, o0, o1), r, w)
 
     def act(out, a, r, w, scale=1.0):
         op("s", lambda: S.activation(out, a, ACT.Copy, scale=scale), r, w)
+
+    def lin(out, a, scale, bias, r, w):
+        op("s", lambda: S.activation(out, a, ACT.Identity, bias=bias, scale=scale), r, w)
+
+    def before(out, junk, off, scale, bias, r, w):
+        op("s", lambda: S.activation(junk, T.tab[:].indirect(off), ACT.Relu, bias=bias, scale=scale, accum_out=out), r, w)
 
     def quant(q, s, a, r, w):
         op("v", lambda: V.quantize_mx(q, s, a), r, w)
@@ -124,10 +132,10 @@ def rank_program(g, core, T, topo):
     def bank(buf, b, n, first=0):
         return buf[:, 512 * b + first:512 * b + first + n]
 
-    dma("y", T.xt[:, 0:1024], T.x[:, 0:1024], (), ["x0"])
+    dma("y", T.xt[:, 0:1024], T.x[:, 0:1024], (), ["x0", "x1"])
     dma("s", T.ut[:], T.u[:], (), ["ut"])
-    dma("s", T.xt[:, 1024:1536], T.x[:, 1024:1536], (), ["x1"])
-    dma("y", T.xt[:, 1536:2048], T.x[:, 1536:2048], (), ["x2"])
+    dma("s", T.xt[:, 1024:1536], T.x[:, 1024:1536], (), ["x2"])
+    dma("y", T.xt[:, 1536:2048], T.x[:, 1536:2048], (), ["x3"])
     dma("s", T.wp[:], T.ws[:], (), ["wp"])
     dma("y", T.wq[:].bitcast(dt.uint8), T.wc[:], (), ["wq"])
     dma("y", T.vt[:], T.v[:], (), ["vt"])
@@ -146,232 +154,223 @@ def rank_program(g, core, T, topo):
         wrote["lp%d" % t] = ("ap%d" % t, k, {}, "far")
         wrote["lq%d" % t] = ("aq%d" % t, k, {}, "far")
 
-    iota(T.pi[:, 4:5], [[0, 1]], 0, 1, ["pi4"], flag=False)
+    iota(T.pi[:, 8:9], [[0, 1]], 0, 1, ["pi8"], flag=False)
     iota(T.jj[:], [[1, 128]], 0, 0, ["jj"])
-    iota(T.r16[:], [[0, 9], [1, 16]], 0, 0, ["r16"])
     iota(T.p4[:], [[16, 2], [0, 2]], 0, 0, ["p4"])
-    iota(T.ct[:], [[1, 16]], 1024, 16, ["ct"])
-    iota(T.d0[:], [[0, CAP], [1, 2]], 0, 0, ["d0"])
-    iota(T.vc[:], [[2, 16], [32, 16]], 1, 0, ["vc"])
+    iota(T.ct[:], [[1, 16]], 1032, 16, ["ct"])
+    iota(T.r4[:], [[0, CAP // 4], [1, 4]], 0, 0, ["r4"])
+    iota(T.vc[:], [[8, 16], [128, 16]], -1024, 0, ["vc"])
     send(T.lp0[:], T.wp[:], "ap0", 0, "wp")
     send(T.lq0[:].bitcast(dt.uint8), T.wq[:].bitcast(dt.uint8), "aq0", 0, "wq")
     send(T.lp1[:], T.wp[:], "ap1", 1, "wp")
     send(T.lq1[:].bitcast(dt.uint8), T.wq[:].bitcast(dt.uint8), "aq1", 1, "wq")
 
     fill(T.eb[:], 0.0, ["eb"])
+    fill(T.lr[:], 0.0, ["lr"])
     fill(T.xs[:, 0:32], -BIG, ["xsl"])
+    p = T.pi[:, 8:9]
+    for k, (shift, bits) in enumerate(((0, 15), (0, 16), (0, 1), (1, 7), (0, 3), (2, 3), (0, 7), (3, 1))):
+        ts(T.pi[:, k:k + 1], p, shift, A.logical_shift_right, ["pi8"], ["pi%d" % k], bits, A.bitwise_and)
     fill(T.xs[:, 544:576], BIG, ["xsr"])
-    fill(T.rr[:, 6:198:6], 1.0, ["rr0"])
-    p = T.pi[:, 4:5]
-    ts(T.pi[:, 0:1], p, 15, A.bitwise_and, ["pi4"], ["pi0"])
-    ts(T.pi[:, 1:2], p, 16, A.bitwise_and, ["pi4"], ["pi1"])
-    ts(T.pi[:, 2:3], p, 1, A.bitwise_and, ["pi4"], ["pi2"])
-    ts(T.pi[:, 3:4], p, 1, A.logical_shift_right, ["pi4"], ["pi3"], 7, A.bitwise_and)
-    cp(T.pf[:, 0:5], T.pi[:, 0:5], ["pi0", "pi1", "pi2", "pi3", "pi4"], ["pf"])
-    piece, half, odd, pair, part = [T.pf[:, i:i + 1] for i in range(5)]
+    cp(T.pf[:, 0:9], T.pi[:, 0:9], ["pi%d" % k for k in range(9)], ["pf"])
+    piece, half, odd, pair, lane, quad, step, oct_, part = [T.pf[:, i:i + 1] for i in range(9)]
+    op("v", lambda: V.memset(T.lr[:, R0 + 6:R0 + 223:6], 1.0), ["lr"], ["rr0"])
     ts(T.eb[:, 3:515:4], T.jj[:], part, A.is_equal, ["jj", "pf", "eb"], ["eb"])
-    ts(T.pc[:, 0:1], piece, 32.0, A.mult, ["pf"], ["pc0"])
-    ts(T.pc[:, 1:2], piece, half, A.add, ["pf"], ["pc1"])
-    ts(T.pc[:, 2:3], odd, 32.0, A.mult, ["pf"], ["pc2"], half, A.add)
+    pc = [T.pc[:, i:i + 1] for i in range(16)]
+    ts(pc[0], piece, 32.0, A.mult, ["pf"], ["pc0"])
     for b in range(4):
         quant(T.qe[:, 128 * b:128 * b + 128], T.se[:, 128 * b:128 * b + 128], T.eb[:, 3 - b:515 - b], ["eb"], ["qe%d" % b])
+    for t in range(ROUNDS):
+        ts(T.offg[:, 6 * t:6 * t + 6], T.jj[:, 0:96:16], pc[0], A.add, ["jj", "pc0"], ["offg%d" % t], float(t), A.add)
+    ts(pc[1], piece, -1.0, A.add, ["pf"], ["pc1"], piece, A.mult)
+    ts(pc[2], odd, 32.0, A.mult, ["pf"], ["pc2"], half, A.add)
+    ts(pc[3], step, 7.0, A.is_equal, ["pf"], ["pc3"], -float(R0 + 6), A.mult)
     quant(T.qu[:], T.su[:], T.ut[:], ["ut"], ["qu"])
 
-    act(T.fp[:, C:4 * FW:FW], T.jj[:, 0:4], ["jj"], ["fz"], 0.0)
-    act(T.dh[:, CAP + 1:4 * DW:DW], T.jj[:, 0:4], ["jj"], ["dz"], 0.0)
-    act(T.dh[:, 0:4 * DW:DW], T.jj[:, 0:4], ["jj"], ["dz0"], 0.0)
-    act(T.ll[:, 0:192:6], T.jj[:, 0:32], ["jj"], ["ll0"], 0.0)
-    act(T.ks[:, 4:5], T.jj[:, 0:1], ["jj"], ["ks0"], 0.0)
-    act(T.loc[:, 0:1], T.jj[:, 0:1], ["jj"], ["loc0"], 0.0)
-    for win, ak in ((T.a0, "a0"), (T.a1, "a1")):
-        act(win[:, 0:CAP], T.r16[:], ["r16"], [ak + "l"], 0.0)
-        act(win[:, CAP:2 * CAP], T.r16[:], ["r16"], [ak], 0.0)
+    for k in range(0, 544, 128):
+        n = min(128, 544 - k)
+        lin(T.tab[:, k:k + n], T.jj[:, 0:n], 1.0, float(k), ["jj"], ["tab%d" % k])
+    tabs = ["tab%d" % k for k in range(0, 544, 128)]
+    lin(pc[4], pc[1], -34.0, -2.0, ["pc1"], ["pc4"])
+    lin(pc[5], piece, -34.0, 511.0, ["pf"], ["pc5"])
+    lin(pc[6], piece, 34.0, -544.0, ["pf"], ["pc6"])
+    lin(pc[7], piece, 68.0, -1088.0, ["pf"], ["pc7"])
+    lin(pc[8], lane, 1.0, 1024.0, ["pf"], ["pc8"])
+    lin(pc[9], pc[1], 17.0, pc[5], ["pc1", "pc5"], ["pc9"])
+    lin(pc[10], step, -5.0, pc[3], ["pf", "pc3"], ["pc10"])
+    act(T.hh[:, 5:204:198], T.jj[:, 0:2], ["jj"], ["hh0"], 0.0)
+    act(T.pm[:], T.jj[:, 0:64], ["jj"], ["pm"], 0.0)
+    lin(pc[11], oct_, 6.0, pc[10], ["pf", "pc10"], ["pc11"])
+    act(T.pd[:, 0:64:4], T.ct[:], ["ct"], ["pd0"], -1.0)
+    act(T.pd[:, 2:64:4], T.ct[:], ["ct"], ["pd2"])
+    lin(T.pm[:, 2:64:4], T.ct[:], 0.0, 1.0, ["ct", "pm"], ["pm2"])
+    act(T.fp[:, 4 * C:4 * C + 4], T.jj[:, 0:4], ["jj"], ["fz"], 0.0)
+    act(T.dh[:, CAP:4 * DW:DW], T.jj[:, 0:4], ["jj"], ["dz"], 0.0)
+    act(T.d0[:, 0:288:2], T.r4[:], ["r4"], ["d0a"], 0.0)
+    lin(T.d0[:, 1:288:2], T.r4[:], 0.0, 4.0, ["r4"], ["d0b"])
+    lin(T.a0[:, 0:288], T.tab[:, 0:288], 0.0, -2048.0, tabs, ["a0"])
+    lin(T.a1[:, 0:288], T.tab[:, 0:288], 0.0, -2048.0, tabs, ["a1"])
+    lin(T.md[:], T.tab[:, 0:256], 0.0, 1.0, tabs, ["md"])
+    act(T.md[:, 7:256:8], T.jj[:, 0:32], ["jj"], ["md"])
 
     tiles = [T.xt, T.t1, T.t2]
     codes = [(T.q0, T.s0), (T.q1, T.s1), (T.q2, T.s2)]
-    pieces = [(0, 256), (256, 384), (384, 512)]
 
-    def quant_piece(t, i, keys):
+    def span(w):
+        return 128 * int(w[0]), 128 * int(w[-1]) + 128
+
+    def quant_piece(t, w):
         q, s = codes[t]
-        a, b = pieces[i]
-        quant(q[:, a:b], s[:, a:b], tiles[t][:, 4 * a:4 * b], keys, ["q%d%d" % (t, i)])
+        a, b = span(w)
+        keys = ["x" + k for k in w] if t == 0 else ["T%d%s" % (j, k) for j in range(4) for k in w]
+        done = ["q%d%s" % (t, k) for k in w]
+        quant(q[:, a:b], s[:, a:b], tiles[t][:, 4 * a:4 * b], keys, done)
         side = (T.qu[:], T.su[:], "qu") if t < ROUNDS else (T.qv[:], T.sv[:], "qv")
-        mm(bank(T.psr, i, b - a), side[0], side[1], q[:, a:b], s[:, a:b], [side[2], "q%d%d" % (t, i)], ["Br%d" % i])
+        mm(bank(T.psr, int(w[0]), b - a), side[0], side[1], q[:, a:b], s[:, a:b], [side[2]] + done, ["Br" + w[0]])
 
-    def turn(i):
-        a, b = pieces[i]
-        tr(T.xs[:, 32 + a:32 + b], bank(T.psr, i, b - a), ["Br%d" % i], ["xs%d" % i])
+    def turn(w):
+        a, b = span(w)
+        tr(T.xs[:, 32 + a:32 + b], bank(T.psr, int(w[0]), b - a), ["Br" + w[0]], ["xs" + k for k in w])
 
-    quant_piece(0, 0, ["x0"])
-    for t in range(ROUNDS):
-        ts(T.offg[:, 6 * t:6 * t + 6], T.jj[:, 0:96:16], T.pc[:, 0:1], A.add, ["jj", "pc0"], ["offg%d" % t], float(t), A.add)
-    ts(T.m1[:], T.jj[:, 0:32], T.pc[:, 1:2], A.is_gt, ["jj", "pc1"], ["m1"])
-    ts(T.m2[:], T.jj[:, 0:32], half, A.subtract, ["jj", "pf"], ["m2"], 16.0, A.is_lt)
-    quant_piece(0, 1, ["x1"])
-    turn(0)
-    quant_piece(0, 2, ["x2"])
-    turn(1)
-    tt(T.msk[:], T.m1[:], T.m2[:], A.mult, ["m1", "m2"], ["msk"])
+    quant_piece(0, "01")
+    ts(T.offf[:], T.jj[:, 0:16:8], pc[2], A.add, ["jj", "pc2", "pf"], ["offf"], pair, A.add)
     ts(T.offr[:], T.p4[:], piece, A.add, ["p4", "pf"], ["offr"])
-    turn(2)
+    quant_piece(0, "2")
+    turn("01")
+    quant_piece(0, "3")
+    turn("2")
+    ts(T.pen[:], T.r4[:], quad, A.is_le, ["r4", "pf"], ["pen"], 4096.0, A.mult)
+    turn("3")
     D = T.dd
     W = [None, T.dd, T.w2, T.w3, T.w4, T.w5]
     wk = [None, "dd", "w2", "w3", "w4", "w5"]
+    ln = T.pd[:, 72:104]
 
     for t in range(ROUNDS):
         last = t + 1 == ROUNDS
         q, s = codes[t]
-        qk = ["q%d%d" % (t, i) for i in range(3)]
+        qk = ["q%d%d" % (t, i) for i in range(4)]
+
+        def plane(b):
+            act(T.fp[:, b:4 * C:4], bank(T.psf, b, C), ["Bf%d" % b], ["f%d" % b])
+
         for b in range(4):
             e = slice(128 * b, 128 * b + 128)
             mm(bank(T.psf, b, C), T.qe[:, e], T.se[:, e], q[:], s[:], qk + ["qe%d" % b], ["Bf%d" % b])
-        for b in range(4):
-            act(T.fp[:, FW * b:FW * b + C], bank(T.psf, b, C), ["Bf%d" % b], ["f%d" % b])
+        for b in range(3):
+            plane(b)
+        cp(T.zz[:], T.xs[:].indirect(T.offg[:, 6 * t:6 * t + 6]), ["xs0", "xs1", "xs2", "xs3", "xsl", "xsr", "offg%d" % t], ["zz"])
         if t == 0:
-            ts(T.offf[:], T.jj[:, 0:16:8], T.pc[:, 2:3], A.add, ["jj", "pc2", "pf"], ["offf"], pair, A.add)
-        cp(T.zz[:], T.xs[:].indirect(T.offg[:, 6 * t:6 * t + 6]), ["xs0", "xs1", "xs2", "xsl", "xsr", "offg%d" % t], ["zz"])
-        if t == 0:
-            ts(T.jc[:], T.jj[:, 0:32], T.pc[:, 0:1], A.add, ["jj", "pc0"], ["jc"])
+            ts(T.offm[:], T.tab[:, 0:192:12], pc[11], A.add, tabs + ["pc11"], ["offm"], float(R0 + 41), A.add)
         tr(D[:], T.zz[:], ["zz"], ["dd"])
-        if t == 0:
-            ts(T.pen[:], T.r16[:], piece, A.is_le, ["r16", "pf"], ["pen"], 1024.0, A.mult)
 
-        def flags(d):
+        def left(d):
             n = 37 if d == 5 else 32
-            o = 1 if d == 5 else 0
-            tt(T.ll[:, 6 - d:6 * n:6], D[:, 32:32 + n], W[d][:, 32 - d:32 + n - d], A.is_lt, ["dd", wk[d]], ["ll%d" % d])
-            tt(T.rr[:, 6 + d - 6 * o:198:6], D[:, 32 - o:64], W[d][:, 33 - o:65], A.is_le, ["dd", wk[d]], ["rr%d" % d])
+            tt(T.lr[:, 6 - d:6 * n:6], D[:, 32:32 + n], W[d][:, 32 - d:32 + n - d], A.is_lt, ["dd", wk[d], "lr"], ["ll%d" % d])
 
-        def above(d):
-            tt(T.kf[:, d - 1:160:5], W[d][:, 32:64], T.m6[:], A.is_gt, [wk[d], "m6"], ["kf%d" % d])
+        def right(d):
+            o = 1 if d == 5 else 0
+            n = 37 - d if last else 32
+            tt(T.lr[:, R0 + 6 + d - 6 * o:R0 + 6 + 6 * n:6], D[:, 32 - o:32 + n], W[d][:, 33 - o:33 + n], A.is_le,
+               ["dd", wk[d], "lr"], ["rr%d" % d])
 
         tt(T.w2[:, 27:68], D[:, 27:68], D[:, 28:69], A.min, ["dd"], ["w2"])
-        flags(1)
+        left(1)
+        right(1)
         tt(T.w4[:, 27:66], T.w2[:, 27:66], T.w2[:, 29:68], A.min, ["w2"], ["w4"])
         tt(T.w3[:, 27:67], T.w2[:, 27:67], D[:, 29:69], A.min, ["w2", "dd"], ["w3"])
-        flags(2)
+        left(2)
         tt(T.w5[:, 27:65], T.w4[:, 27:65], D[:, 31:69], A.min, ["w4", "dd"], ["w5"])
-        flags(3)
-        flags(4)
-        flags(5)
-        if last:
-            tt(T.m6[:], T.w5[:, 32:64], D[:, 37:69], A.min, ["w5", "dd"], ["m6"])
-        scan(T.hh[:], T.ll[:, 0:192], T.rr[:, 6:198], 0.0, A.mult, A.max,
-             ["ll%d" % d for d in range(6)] + ["rr%d" % d for d in range(6)], ["hh"])
-        tt(T.ch[:], T.rr[:, 5:197:6], T.ll[:, 31:222:6], A.max, ["rr5", "ll5"], ["ch"])
-        scan(T.loc[:, 1:33], T.hh[:, 5:192:6], T.hh[:, 5:192:6], 0.0, A.add, A.max, ["hh"], ["loc"])
-        scan(T.ln[:], T.ch[:], T.ch[:], 0.0, A.add, A.max, ["ch"], ["ln"])
-        ts(T.mt[:], T.msk[:], T.loc[:, 32:33], A.mult, ["msk", "loc"], ["mt"], 2.0, A.mult)
-        tt(T.nn[:], T.loc[:, 0:32:2], T.loc[:, 2:34:2], A.is_equal, ["loc", "loc0"], ["nn"])
-        tr(T.mtt[:], T.mt[:], ["mt"], ["mtt"])
-        tt(T.qq[:], T.nn[:], T.ct[:], A.mult, ["nn", "ct"], ["qq"])
-        tt(T.pp[:], T.loc[:, 0:32:2], T.loc[:, 1:33:2], A.add, ["loc", "loc0"], ["pp"])
-        total(T.base[:, 0:1], T.mtt[:], ["mtt"], ["base"])
-        tt(T.pl[:], T.pp[:], T.qq[:], A.add, ["pp", "qq"], ["pl"])
-        ts(T.nt[:], T.msk[:], T.ln[:, 31:32], A.mult, ["msk", "ln"], ["nt"])
-        ts(T.offs[:], T.pl[:], T.base[:, 0:1], A.add, ["pl", "base"], ["offs"])
-        tr(T.ntt[:], T.nt[:], ["nt"], ["ntt"])
+        right(2)
+        left(4)
+        left(5)
+        right(5)
+        right(4)
+        left(3)
+        right(3)
+        tt(T.ch[:], T.lr[:, R0 + 5:R0 + 197:6], T.lr[:, 31:222:6], A.max, ["rr5", "ll5"], ["ch"])
+        flags = ["ll%d" % d for d in range(1, 6)] + ["rr%d" % d for d in range(6)]
+        scan(T.hh[:, 6:198], T.lr[:, 0:192], T.lr[:, R0 + 6:R0 + 198], 0.0, A.mult, A.max, flags, ["hh"])
+        scan(ln, T.ch[:], T.ch[:], pc[4], A.add, A.add, ["ch", "pc4"], ["ln"])
+        scan(T.pd[:, 1:66:2], T.hh[:, 5:203:6], T.hh[:, 11:204:6], pc[4], A.add, A.add, ["hh", "hh0", "pc4"], ["yy"])
+        tt(T.pm[:, 1:64:4], T.hh[:, 11:200:12], T.hh[:, 17:204:12], A.max, ["hh", "pm"], ["or"])
+        ts(T.offb[:, 0:3:2], T.pd[:, 65:104:38], 0.5, A.mult, ["yy", "ln", "pc9"], ["offb"], pc[9], A.add)
+        scan(T.pl[:], T.pm[:], T.pd[:, 0:64], 0.0, A.mult, A.add, ["or", "yy", "pm", "pm2", "pd0", "pd2"], ["pl"])
+        before(T.base[:, 0:1], T.j0[:], T.offb[:, 0:1], 2.0, pc[7], tabs + ["offb", "pc7"], ["base"])
+        before(T.nb[:, 0:1], T.j1[:], T.offb[:, 2:3], 1.0, pc[6], tabs + ["offb", "pc6"], ["nb"])
+        plane(3)
+        ts(T.offs[:], T.pl[:, 2:64:4], T.base[:, 0:1], A.add, ["pl", "base"], ["offs"], 2.0, A.add)
         win, ak = [T.a0, T.a1][t], "a%d" % t
-        cp(win[:].indirect(T.offs[:]), T.vc[:], ["offs", "vc"], [ak, ak + "l"])
-        total(T.nb[:, 0:1], T.ntt[:], ["ntt"], ["nb"])
-        scan(T.e1[:], T.d0[:], win[:, 0:288], 0.0, A.add, A.max, ["d0", ak], ["e1"])
+        cp(win[:].indirect(T.offs[:]), T.vc[:], ["offs", "vc"], [ak])
+        lin(T.n2[:], ln.indirect(T.offr[:]), 0.5, T.nb[:, 0:1], ["ln", "offr", "nb"], ["n2"])
         if last:
-            above(1)
+            lin(T.oln[:], ln, 0.5, T.nb[:, 0:1], ["ln", "nb"], ["oln"])
+            dma("y", T.ol[:, C:2 * C], T.oln[:], ["oln"], [])
+            lin(T.mg[:], T.lr[:].indirect(T.offm[:]), -1.0, 1.0, flags + ["offm", "lr"], ["mg"])
+        scan(T.e1[:], T.d0[:], win[:, 0:288], -4096.0, A.add, A.max, ["d0a", "d0b", ak], ["e1"])
+        tr(T.n2t[:], T.n2[:], ["n2"], ["n2t"])
         scan(T.e2[:], T.pen[:], T.e1[:, 1:288:2], 0.0, A.add, A.min, ["pen", "e1"], ["e2"])
-        if last:
-            above(2)
-        ts(T.offp[:, 0:9], T.e2[:, 15:CAP:16], -1.0, A.add, ["e2"], ["offp"], float(C), A.min)
-        if last:
-            above(3)
-        for b in range(4):
-            src = T.fp[:, FW * b:FW * b + C + 1].indirect(T.offp[:, 0:9])
-            (cp if b < 2 else act)(T.pt[:, b:4 * CAP:4], src, ["f%d" % b, "fz", "offp"], ["p%d" % b])
-        if last:
-            above(4)
-        quant(T.qp[:], T.sp[:], T.pt[:], ["p0", "p1", "p2", "p3"], ["qp"])
+        ts(T.offn[:], T.n2t[:].indirect(T.offf[:]), float(CAP), A.min, ["n2t", "offf"], ["offn"])
+        ts(T.offp[:], T.e2[:, 3:CAP:4], 1024.0, A.min, ["e2", "pc8"], ["offp"], pc[8], A.add)
+        fk = ["f0", "f1", "f2", "f3", "fz", "offp"]
+        cp(T.pt[:, 0:288], T.fp[:, 0:4 * C + 4].indirect(T.offp[:, 0:18]), fk, ["p0"])
+        act(T.pt[:, 288:576], T.fp[:, 0:4 * C + 4].indirect(T.offp[:, 18:36]), fk, ["p1"])
+        quant(T.qp[:], T.sp[:], T.pt[:], ["p0", "p1"], ["qp"])
         lq, lp = [(T.lq0, T.lp0), (T.lq1, T.lp1)][t]
         for b in (2, 0, 3, 1):
             e = slice(128 * b, 128 * b + 128)
             mm(bank(T.psr, b, CAP), lq[:, e], lp[:, e], T.qp[:], T.sp[:], ["qp", "lq%d" % t, "lp%d" % t], ["Br%d" % b])
-        ts(T.n2[:], T.ln[:].indirect(T.offr[:]), T.nb[:, 0:1], A.add, ["ln", "offr", "nb"], ["n2"], float(CAP + 1), A.min)
         if last:
-            above(5)
-        tr(T.n2t[:], T.n2[:], ["n2"], ["n2t"])
+            scan(T.mk[:], T.md[:], T.mg[:], 0.0, A.add, A.mult, ["mg", "md"], ["mk"])
+        else:
+            quant(T.qv[:], T.sv[:], T.vt[:], ["vt"], ["qv"])
         for b in (2, 0, 3, 1):
             if b < 2:
                 ts(T.ht[:, b:4 * CAP:4], bank(T.psr, b, CAP), 0.03125, A.mult, ["Br%d" % b], ["h%d" % b])
             else:
                 act(T.ht[:, b:4 * CAP:4], bank(T.psr, b, CAP), ["Br%d" % b], ["h%d" % b], 0.03125)
-        if last:
-            ts(T.oln[:], T.ln[:], T.nb[:, 0:1], A.add, ["ln", "nb"], ["oln"], -1.0, A.add)
-            dma("y", T.ol[:, C:2 * C], T.oln[:], ["oln"], [])
         quant(T.qh[:], T.sh[:], T.ht[:], ["h0", "h1", "h2", "h3"], ["qh"])
-        for b in (0, 2, 1, 3):
+        for b in range(4):
             e = slice(128 * b, 128 * b + 128)
             mm(bank(T.psr, b, CAP), T.qe[:, e], T.se[:, e], T.qh[:], T.sh[:], ["qh", "qe%d" % b], ["Br%d" % b])
-        cp(T.offn[:], T.n2t[:].indirect(T.offf[:]), ["n2t", "offf"], ["offn"])
         if last:
-            scan(T.ks[:, 5:165], T.kf[:], T.kf[:], 0.0, A.add, A.max, ["kf%d" % d for d in range(1, 6)], ["ks"])
-        else:
-            quant(T.qv[:], T.sv[:], T.vt[:], ["vt"], ["qv"])
+            lin(T.olm[:], T.mk[:, 7:256:8], 1.0, pc[0], ["mk", "pc0"], ["olm"])
+            dma("y", T.ol[:, 0:C], T.olm[:], ["olm"], [])
 
         new = tiles[t + 1]
-
-        def held(b, by):
-            by(T.dh[:, DW * b + 1:DW * b + 1 + CAP], bank(T.psr, b, CAP), ["Br%d" % b], ["dh%d" % b])
-
-        def came(b, h):
-            return T.dh[:, DW * b:DW * b + CAP + 2].indirect(T.offn[:, 16 * h:16 * h + 16])
-
-        def fetch(b, h):
-            act(T.gb[:, 512 * b + 256 * h:512 * b + 256 * h + 256], came(b, h), ["dh%d" % b, "dz", "dz0", "offn"], ["g%d%d" % (b, h)])
-
-        def add(b, h, direct):
-            out = new[:, 1024 * h + b:1024 * h + 1024:4]
-            key = ["T%d%d" % (h, b)]
-            if direct:
-                tt(out, came(b, h), T.fp[:, FW * b + 256 * h:FW * b + 256 * h + 256], A.add, ["dh%d" % b, "dz", "dz0", "offn", "f%d" % b], key)
+        for word in PLAN[t].split():
+            kind = word[0]
+            if kind == "q":
+                quant_piece(t + 1, word[1:])
+            elif kind == "t":
+                turn(word[1:])
+            elif kind == "c":
+                a, z = span(word[1:])
+                dma("y", T.oc[:, 4 * a:4 * z], T.q2[:, a:z].bitcast(dt.uint8), ["q2" + k for k in word[1:]], [])
+            elif kind == "y":
+                w = word[1:-1]
+                a, z = span(w)
+                if w[-1] == "3":
+                    for k in range(4):
+                        dma("ys"[k % 2], T.osc[4 * k:4 * k + 4, :], T.s2[32 * k:32 * k + 4, :], ["q20", "q21", "q22", "q23"], [])
+                (cp if word[-1] == "v" else act)(T.ysb[:, a:z], bank(T.psr, int(w[0]), z - a), ["Br" + w[0]], ["y" + w])
+                dma("s" if w[-1] == "3" else "y", T.y[:, a:z], T.ysb[:, a:z], ["y" + w], [])
+            elif kind == "h":
+                b = int(word[1])
+                (cp if word[2] == "v" else act)(T.dh[:, DW * b:DW * b + CAP], bank(T.psr, b, CAP), ["Br%d" % b], ["dh%d" % b])
             else:
-                tt(out, bank(T.psf, b, 256, 256 * h), T.gb[:, 512 * b + 256 * h:512 * b + 256 * h + 256], A.add, ["Bf%d" % b, "g%d%d" % (b, h)], key)
-
-        held(0, cp)
-        held(2, act)
-        held(1, act)
-        fetch(2, 0)
-        held(3, act)
-        fetch(3, 0)
-        fetch(1, 1)
-        fetch(2, 1)
-        fetch(3, 1)
-        if last:
-            tt(T.kd[:], T.ks[:, 9:165:5], T.ks[:, 4:160:5], A.subtract, ["ks", "ks0"], ["kd"])
-        for b in range(4):
-            add(b, 0, b < 2)
-        add(0, 1, True)
-        quant_piece(t + 1, 0, ["T0%d" % b for b in range(4)])
-        if last:
-            dma("y", T.oc[:, 0:1024], T.q2[:, 0:256].bitcast(dt.uint8), ["q20"], [])
-            act(T.ysb[:, 0:256], bank(T.psr, 0, 256), ["Br0"], ["y0"])
-        for b in range(1, 4):
-            add(b, 1, False)
-        if last:
-            tt(T.olm[:], T.kd[:], T.jc[:], A.add, ["kd", "jc"], ["olm"])
-            dma("y", T.y[:, 0:256], T.ysb[:, 0:256], ["y0"], [])
-            dma("y", T.ol[:, 0:C], T.olm[:], ["olm"], [])
-        else:
-            turn(0)
-        quant_piece(t + 1, 1, ["T1%d" % b for b in range(4)])
-        quant_piece(t + 1, 2, ["T1%d" % b for b in range(4)])
-        if not last:
-            turn(1)
-            turn(2)
-
-    act(T.ysb[:, 256:384], bank(T.psr, 1, 128), ["Br1"], ["y1"])
-    cp(T.ysb[:, 384:512], bank(T.psr, 2, 128), ["Br2"], ["y2"])
-    dma("y", T.oc[:, 1024:2048], T.q2[:, 256:512].bitcast(dt.uint8), ["q21", "q22"], [])
-    dma("s", T.y[:, 256:512], T.ysb[:, 256:512], ["y1", "y2"], [])
-    for k in range(4):
-        dma("y" if k < 3 else "s", T.osc[4 * k:4 * k + 4, :], T.s2[32 * k:32 * k + 4, :], ["q20", "q21", "q22"], [])
+                b, w = int(word[1]), word[2:]
+                a, z = span(w)
+                came = T.dh[:, DW * b:DW * b + CAP + 1].indirect(T.offn[:, a // 16:z // 16])
+                got = T.gb[:, 512 * b + a:512 * b + z]
+                out = new[:, 4 * a + b:4 * z:4]
+                gk, tk = ["g%d%s" % (b, k) for k in w], ["T%d%s" % (b, k) for k in w]
+                if kind == "f":
+                    act(got, came, ["dh%d" % b, "dz", "offn"], gk)
+                elif kind == "d":
+                    tt(out, came, T.fp[:, 4 * a + b:4 * z:4], A.add, ["dh%d" % b, "dz", "offn", "f%d" % b], tk)
+                else:
+                    tt(out, bank(T.psf, b, z - a, a), got, A.add, ["Bf%d" % b] + gk, tk)
 
     g.wait_ge(T.sem.sent, sent[0])
     for sem, val in count.items():

@@ -4,27 +4,33 @@ C, CAP, ROUNDS = 512, 144, 2
 BIG = 1.0e29
 DW = 160
 R0 = 224
+PV = 18
 F32, BF, U16, I32, X4, U8 = "float32", "bfloat16", "uint16", "int32", "float8_e4m3fn_x4", "uint8"
 SCRATCH = {"psf": ("psum", [128, 2048], F32), "psr": ("psum", [128, 2048], F32)}
 for _d, _l in (
-    (BF, "xt 2048 ut 512 vt 512 t1 2048 t2 2048 eb 520 fp 2064 dh 640 gb 2048 pt 576 ht 576 lr 464 hh 208 "
+    (BF, "xt 2048 ut 512 vt 512 t1 2048 t2 2048 eb 520 eo 520 fp 2064 dh 640 gb 2048 pt 576 ht 592 lr 464 hh 208 "
          "a0 4128 a1 4128 vc 256 d0 288 e1 288 e2 144 pen 144 mg 256 md 256 mk 256"),
-    (X4, "q0 512 q1 512 q2 512 qu 128 qv 128 wq 512 lq0 512 lq1 512 qe 512 qp 144 qh 144"),
-    (U8, "s0 512 s1 512 s2 512 su 128 sv 128 wp 512 lp0 512 lp1 512 se 512 sp 144 sh 144"),
+    (X4, "q0 512 q1 512 q2 512 qu 128 qv 128 wq 512 lq0 512 lq1 512 qe 512 qo 512 qp 144 qh 146 "
+         "pa0 128 pb0 128 pa1 128 pb1 128"),
+    (U8, "s0 512 s1 512 s2 512 su 128 sv 128 wp 512 lp0 512 lp1 512 se 512 so 512 sp 144 sh 146 "
+         "sa0 128 sb0 128 sa1 128 sb1 128"),
     (I32, "pi 12"),
-    (U16, "offg 12 offr 4 offf 2 offs 16 offp 36 offn 32 offb 4 offm 16"),
-    (F32, "ysb 512 olm 32 oln 32 jj 128 pf 12 pc 16 r4 144 ct 16 p4 4 tab 544 xs 576 zz 96 dd 96 w2 72 w3 72 w4 72 w5 72 "
-          "pd 104 pm 64 pl 64 ch 32 base 2 nb 2 j0 16 j1 16 n2 64 n2t 64"),
+    (U16, "offg 12 offr 4 offf 2 offs 16 offp 36 offn 32 offb 2 offm 16 offa 16 offo 16 offe 2"),
+    (F32, "ysb 512 olm 32 oln 32 jj 128 pf 12 pc 16 r4 144 ct 16 p4 4 tab 544 xs 576 zz 96 ww 480 "
+          "pd 64 pm 64 pl 64 ch 32 ln 32 gt 8 dl 8 base 2 nb 2 j0 16 j1 16 n2 64 n2t 64"),
 ):
     _w = _l.split()
     for _i in range(0, len(_w), 2):
         SCRATCH[_w[_i]] = ("sbuf", [128, int(_w[_i + 1])], _d)
 SEMAPHORES = ["cv", "cs", "cp", "cg", "sent", "ap0", "aq0", "ap1", "aq1", "stored"] + ["d%d" % i for i in range(10)]
 
+LISTS = ("f0 f1 c2 w2 l1 r1 l2 w4 w3 l3 r2 w5 l4 r4 r3 l5 r5 gt ch hh ln or ob bs nb n2 f2 f3 g0 g1 g2 g3 yy dl c1 pl of "
+         "sc ol e1 nt e2 on op oa pv ps oo")
 PLAN = [
-    "h0v h1s h2s h3s d00123 f20123 d3012 f1012 a20123 f13 a1012 f33 a13 q01 a33 q2 q3 t01 t2 t3",
-    "h0v h1s h2s h3s d0012 f20 d301 f10 f11 f12 a20 a10 a11 q0 c0 d21 f32 a32 a12 f22 y0s a22 q1 c1 f23 q2 c2 f13 d33 "
-    "y1s d03 a23 y2s a13 q3 c3 y3v",
+    "PA m1 SBs m2 m0 PB m3 h1s SAs E3 h2v h3s f21 d1123 h0s d323 d023 f223 E2 a21 E0 f01 a223 k3s f31 a01 a31 E1 k1s "
+    "k2s q2 q3 k0s q1 q0 t2 t3 t1 t0",
+    "m2 SAs SBs m0 m3 PA h2v PB d2123 m1 E3 h0s h3s E1 h1s f31 E0 E2 d01 a31 f11 f023 k3s a11 d32 k0s q1 k1s c1y k2s "
+    "f33 d123 q0 a02 a33 a03 c0y y1s q2 z1y q3 y0v c2s c3s o1y y2v o2s z0s o0y z2y y3v z3y o3s",
 ]
 
 
@@ -53,14 +59,14 @@ def rank_program(g, core, T, topo):
                     if known[e].get(k, 0) < x:
                         known[e][k] = x
 
-    def op(e, call, r=(), w=(), dma=False):
+    def op(e, call, r=(), w=(), dma=False, adds=False):
         marks = []
         for k in r:
             marks.append(wrote[k])
             if k[0] == "B":
                 marks += [m for m in read.get(k, []) if m[3] != e]
         for k in w:
-            if k in wrote:
+            if k in wrote and not adds:
                 marks.append(wrote[k])
             marks += read.get(k, [])
         need(e, marks)
@@ -111,14 +117,14 @@ def rank_program(g, core, T, topo):
     def lin(out, a, scale, bias, r, w):
         op("s", lambda: S.activation(out, a, ACT.Identity, bias=bias, scale=scale), r, w)
 
-    def before(out, junk, off, scale, bias, r, w):
-        op("s", lambda: S.activation(junk, T.tab[:].indirect(off), ACT.Relu, bias=bias, scale=scale, accum_out=out), r, w)
+    def before(out, junk, scale, bias, r, w):
+        op("s", lambda: S.activation(junk, T.tab[:].indirect(T.offb[:, 0:1]), ACT.Relu, bias=bias, scale=scale, accum_out=out), r, w)
 
     def quant(q, s, a, r, w):
         op("v", lambda: V.quantize_mx(q, s, a), r, w)
 
-    def mm(out, lq, ls, rq, rs, r, w):
-        op("p", lambda: g.tensor.matmul_mx(out, lq, ls, rq, rs, True, True), r, w)
+    def mm(out, lq, ls, rq, rs, r, w, stop=True):
+        op("p", lambda: g.tensor.matmul_mx(out, lq, ls, rq, rs, True, stop), r, w)
 
     def iota(out, pattern, base, cm, w, flag=True):
         if flag:
@@ -158,7 +164,7 @@ def rank_program(g, core, T, topo):
     iota(T.jj[:], [[1, 128]], 0, 0, ["jj"])
     iota(T.p4[:], [[16, 2], [0, 2]], 0, 0, ["p4"])
     iota(T.ct[:], [[1, 16]], 1032, 16, ["ct"])
-    iota(T.r4[:], [[0, CAP // 4], [1, 4]], 0, 0, ["r4"])
+    iota(T.r4[:], [[0, CAP // 4], [4, 4]], 0, 0, ["r4"])
     iota(T.vc[:], [[8, 16], [128, 16]], -1024, 0, ["vc"])
     send(T.lp0[:], T.wp[:], "ap0", 0, "wp")
     send(T.lq0[:].bitcast(dt.uint8), T.wq[:].bitcast(dt.uint8), "aq0", 0, "wq")
@@ -166,52 +172,56 @@ def rank_program(g, core, T, topo):
     send(T.lq1[:].bitcast(dt.uint8), T.wq[:].bitcast(dt.uint8), "aq1", 1, "wq")
 
     fill(T.eb[:], 0.0, ["eb"])
-    fill(T.lr[:], 0.0, ["lr"])
-    fill(T.xs[:, 0:32], -BIG, ["xsl"])
     p = T.pi[:, 8:9]
-    for k, (shift, bits) in enumerate(((0, 15), (0, 16), (0, 1), (1, 7), (0, 3), (2, 3), (0, 7), (3, 1))):
-        ts(T.pi[:, k:k + 1], p, shift, A.logical_shift_right, ["pi8"], ["pi%d" % k], bits, A.bitwise_and)
+    for k, bits in enumerate((15, 16, 1, 3, 7)):
+        ts(T.pi[:, k:k + 1], p, bits, A.bitwise_and, ["pi8"], ["pi%d" % k])
+    fill(T.xs[:, 0:32], -BIG, ["xsl"])
+    cp(T.pf[:, 8:9], p, ["pi8"], ["pf8"])
+    cp(T.pf[:, 0:5], T.pi[:, 0:5], ["pi%d" % k for k in range(5)], ["pf"])
+    piece, half, odd, lane, step = [T.pf[:, i:i + 1] for i in range(5)]
     fill(T.xs[:, 544:576], BIG, ["xsr"])
-    cp(T.pf[:, 0:9], T.pi[:, 0:9], ["pi%d" % k for k in range(9)], ["pf"])
-    piece, half, odd, pair, lane, quad, step, oct_, part = [T.pf[:, i:i + 1] for i in range(9)]
-    op("v", lambda: V.memset(T.lr[:, R0 + 6:R0 + 223:6], 1.0), ["lr"], ["rr0"])
-    ts(T.eb[:, 3:515:4], T.jj[:], part, A.is_equal, ["jj", "pf", "eb"], ["eb"])
+    ts(T.eb[:, 3:515:4], T.jj[:], T.pf[:, 8:9], A.is_equal, ["jj", "pf8", "eb"], ["eb"])
     pc = [T.pc[:, i:i + 1] for i in range(16)]
-    ts(pc[0], piece, 32.0, A.mult, ["pf"], ["pc0"])
+    ts(pc[1], piece, -1.0, A.add, ["pf"], ["pc1"], piece, A.mult)
+    ts(pc[3], step, 7.0, A.is_equal, ["pf"], ["pc3"], -float(R0 + 6), A.mult)
     for b in range(4):
         quant(T.qe[:, 128 * b:128 * b + 128], T.se[:, 128 * b:128 * b + 128], T.eb[:, 3 - b:515 - b], ["eb"], ["qe%d" % b])
-    for t in range(ROUNDS):
-        ts(T.offg[:, 6 * t:6 * t + 6], T.jj[:, 0:96:16], pc[0], A.add, ["jj", "pc0"], ["offg%d" % t], float(t), A.add)
-    ts(pc[1], piece, -1.0, A.add, ["pf"], ["pc1"], piece, A.mult)
-    ts(pc[2], odd, 32.0, A.mult, ["pf"], ["pc2"], half, A.add)
-    ts(pc[3], step, 7.0, A.is_equal, ["pf"], ["pc3"], -float(R0 + 6), A.mult)
     quant(T.qu[:], T.su[:], T.ut[:], ["ut"], ["qu"])
 
     for k in range(0, 544, 128):
         n = min(128, 544 - k)
         lin(T.tab[:, k:k + n], T.jj[:, 0:n], 1.0, float(k), ["jj"], ["tab%d" % k])
     tabs = ["tab%d" % k for k in range(0, 544, 128)]
-    lin(pc[4], pc[1], -34.0, -2.0, ["pc1"], ["pc4"])
+    lin(pc[0], piece, 32.0, 0.0, ["pf"], ["pc0"])
+    lin(pc[2], odd, 31.5, half, ["pf"], ["pc2"])
+    lin(pc[12], lane, -1.0, piece, ["pf"], ["pc12"])
+    lin(pc[10], step, -5.75, pc[3], ["pf", "pc3"], ["pc10"])
     lin(pc[5], piece, -34.0, 511.0, ["pf"], ["pc5"])
+    act(T.lr[:], T.tab[:, 0:464], tabs, ["lr"], 0.0)
+    act(T.pm[:], T.jj[:, 0:64], ["jj"], ["pm"], 0.0)
+    lin(pc[13], piece, 0.5, pc[2], ["pf", "pc2"], ["pc13"])
+    lin(pc[11], piece, 0.75, pc[10], ["pf", "pc10"], ["pc11"])
+    lin(pc[4], pc[1], -34.0, -2.0, ["pc1"], ["pc4"])
     lin(pc[6], piece, 34.0, -544.0, ["pf"], ["pc6"])
     lin(pc[7], piece, 68.0, -1088.0, ["pf"], ["pc7"])
     lin(pc[8], lane, 1.0, 1024.0, ["pf"], ["pc8"])
     lin(pc[9], pc[1], 17.0, pc[5], ["pc1", "pc5"], ["pc9"])
-    lin(pc[10], step, -5.0, pc[3], ["pf", "pc3"], ["pc10"])
-    act(T.hh[:, 5:204:198], T.jj[:, 0:2], ["jj"], ["hh0"], 0.0)
-    act(T.pm[:], T.jj[:, 0:64], ["jj"], ["pm"], 0.0)
-    lin(pc[11], oct_, 6.0, pc[10], ["pf", "pc10"], ["pc11"])
+    lin(T.pf[:, 9:10], half, -1.0, pc[13], ["pf", "pc13"], ["pf9"])
+    lin(T.lr[:, R0 + 6:R0 + 223:6], T.jj[:, 0:37], 0.0, 1.0, ["jj", "lr"], ["rr0"])
+    act(T.hh[:, 5:6], T.jj[:, 0:1], ["jj"], ["hh0"], 0.0)
+    lin(T.gt[:, 5:6], T.jj[:, 0:1], 0.0, 2.0, ["jj"], ["gt5"])
     act(T.pd[:, 0:64:4], T.ct[:], ["ct"], ["pd0"], -1.0)
     act(T.pd[:, 2:64:4], T.ct[:], ["ct"], ["pd2"])
     lin(T.pm[:, 2:64:4], T.ct[:], 0.0, 1.0, ["ct", "pm"], ["pm2"])
     act(T.fp[:, 4 * C:4 * C + 4], T.jj[:, 0:4], ["jj"], ["fz"], 0.0)
     act(T.dh[:, CAP:4 * DW:DW], T.jj[:, 0:4], ["jj"], ["dz"], 0.0)
+    act(T.ht[:, 576:584], T.jj[:, 0:8], ["jj"], ["hz"], 0.0)
+    lin(pc[14], half, 64.0, T.pf[:, 8:9], ["pf", "pf8"], ["pc14"])
+    lin(pc[15], half, 9.0, 0.0, ["pf"], ["pc15"])
     act(T.d0[:, 0:288:2], T.r4[:], ["r4"], ["d0a"], 0.0)
     lin(T.d0[:, 1:288:2], T.r4[:], 0.0, 4.0, ["r4"], ["d0b"])
     lin(T.a0[:, 0:288], T.tab[:, 0:288], 0.0, -2048.0, tabs, ["a0"])
-    lin(T.a1[:, 0:288], T.tab[:, 0:288], 0.0, -2048.0, tabs, ["a1"])
-    lin(T.md[:], T.tab[:, 0:256], 0.0, 1.0, tabs, ["md"])
-    act(T.md[:, 7:256:8], T.jj[:, 0:32], ["jj"], ["md"])
+    act(T.eo[:], T.tab[:, 0:520], tabs, ["eo"], 0.0)
 
     tiles = [T.xt, T.t1, T.t2]
     codes = [(T.q0, T.s0), (T.q1, T.s1), (T.q2, T.s2)]
@@ -233,128 +243,169 @@ def rank_program(g, core, T, topo):
         tr(T.xs[:, 32 + a:32 + b], bank(T.psr, int(w[0]), b - a), ["Br" + w[0]], ["xs" + k for k in w])
 
     quant_piece(0, "01")
-    ts(T.offf[:], T.jj[:, 0:16:8], pc[2], A.add, ["jj", "pc2", "pf"], ["offf"], pair, A.add)
-    ts(T.offr[:], T.p4[:], piece, A.add, ["p4", "pf"], ["offr"])
+    for t in range(ROUNDS):
+        ts(T.offg[:, 6 * t:6 * t + 6], T.jj[:, 0:96:16], pc[0], A.add, ["jj", "pc0"], ["offg%d" % t], float(t), A.add)
     quant_piece(0, "2")
     turn("01")
+    ts(T.offf[:], T.jj[:, 0:16:8], pc[13], A.add, ["jj", "pc13"], ["offf"])
+    ts(T.offr[:], T.p4[:], piece, A.add, ["p4", "pf"], ["offr"])
     quant_piece(0, "3")
     turn("2")
-    ts(T.pen[:], T.r4[:], quad, A.is_le, ["r4", "pf"], ["pen"], 4096.0, A.mult)
+    ts(T.pen[:], T.r4[:], pc[12], A.is_le, ["r4", "pc12"], ["pen"], 4096.0, A.mult)
     turn("3")
-    D = T.dd
-    W = [None, T.dd, T.w2, T.w3, T.w4, T.w5]
-    wk = [None, "dd", "w2", "w3", "w4", "w5"]
-    ln = T.pd[:, 72:104]
+
+    def W(d, a, b):
+        return T.ww[:, 96 * (5 - d) + a:96 * (5 - d) + b]
 
     for t in range(ROUNDS):
         last = t + 1 == ROUNDS
         q, s = codes[t]
         qk = ["q%d%d" % (t, i) for i in range(4)]
-
-        def plane(b):
-            act(T.fp[:, b:4 * C:4], bank(T.psf, b, C), ["Bf%d" % b], ["f%d" % b])
-
         for b in range(4):
             e = slice(128 * b, 128 * b + 128)
             mm(bank(T.psf, b, C), T.qe[:, e], T.se[:, e], q[:], s[:], qk + ["qe%d" % b], ["Bf%d" % b])
-        for b in range(3):
-            plane(b)
         cp(T.zz[:], T.xs[:].indirect(T.offg[:, 6 * t:6 * t + 6]), ["xs0", "xs1", "xs2", "xs3", "xsl", "xsr", "offg%d" % t], ["zz"])
         if t == 0:
             ts(T.offm[:], T.tab[:, 0:192:12], pc[11], A.add, tabs + ["pc11"], ["offm"], float(R0 + 41), A.add)
-        tr(D[:], T.zz[:], ["zz"], ["dd"])
-
-        def left(d):
-            n = 37 if d == 5 else 32
-            tt(T.lr[:, 6 - d:6 * n:6], D[:, 32:32 + n], W[d][:, 32 - d:32 + n - d], A.is_lt, ["dd", wk[d], "lr"], ["ll%d" % d])
-
-        def right(d):
-            o = 1 if d == 5 else 0
-            n = 37 - d if last else 32
-            tt(T.lr[:, R0 + 6 + d - 6 * o:R0 + 6 + 6 * n:6], D[:, 32 - o:32 + n], W[d][:, 33 - o:33 + n], A.is_le,
-               ["dd", wk[d], "lr"], ["rr%d" % d])
-
-        tt(T.w2[:, 27:68], D[:, 27:68], D[:, 28:69], A.min, ["dd"], ["w2"])
-        left(1)
-        right(1)
-        tt(T.w4[:, 27:66], T.w2[:, 27:66], T.w2[:, 29:68], A.min, ["w2"], ["w4"])
-        tt(T.w3[:, 27:67], T.w2[:, 27:67], D[:, 29:69], A.min, ["w2", "dd"], ["w3"])
-        left(2)
-        tt(T.w5[:, 27:65], T.w4[:, 27:65], D[:, 31:69], A.min, ["w4", "dd"], ["w5"])
-        right(2)
-        left(4)
-        left(5)
-        right(5)
-        right(4)
-        left(3)
-        right(3)
-        tt(T.ch[:], T.lr[:, R0 + 5:R0 + 197:6], T.lr[:, 31:222:6], A.max, ["rr5", "ll5"], ["ch"])
-        flags = ["ll%d" % d for d in range(1, 6)] + ["rr%d" % d for d in range(6)]
-        scan(T.hh[:, 6:198], T.lr[:, 0:192], T.lr[:, R0 + 6:R0 + 198], 0.0, A.mult, A.max, flags, ["hh"])
-        scan(ln, T.ch[:], T.ch[:], pc[4], A.add, A.add, ["ch", "pc4"], ["ln"])
-        scan(T.pd[:, 1:66:2], T.hh[:, 5:203:6], T.hh[:, 11:204:6], pc[4], A.add, A.add, ["hh", "hh0", "pc4"], ["yy"])
-        tt(T.pm[:, 1:64:4], T.hh[:, 11:200:12], T.hh[:, 17:204:12], A.max, ["hh", "pm"], ["or"])
-        ts(T.offb[:, 0:3:2], T.pd[:, 65:104:38], 0.5, A.mult, ["yy", "ln", "pc9"], ["offb"], pc[9], A.add)
-        scan(T.pl[:], T.pm[:], T.pd[:, 0:64], 0.0, A.mult, A.add, ["or", "yy", "pm", "pm2", "pd0", "pd2"], ["pl"])
-        before(T.base[:, 0:1], T.j0[:], T.offb[:, 0:1], 2.0, pc[7], tabs + ["offb", "pc7"], ["base"])
-        before(T.nb[:, 0:1], T.j1[:], T.offb[:, 2:3], 1.0, pc[6], tabs + ["offb", "pc6"], ["nb"])
-        plane(3)
-        ts(T.offs[:], T.pl[:, 2:64:4], T.base[:, 0:1], A.add, ["pl", "base"], ["offs"], 2.0, A.add)
+        tr(W(1, 0, 96), T.zz[:], ["zz"], ["w1"])
         win, ak = [T.a0, T.a1][t], "a%d" % t
-        cp(win[:].indirect(T.offs[:]), T.vc[:], ["offs", "vc"], [ak])
-        lin(T.n2[:], ln.indirect(T.offr[:]), 0.5, T.nb[:, 0:1], ["ln", "offr", "nb"], ["n2"])
-        if last:
-            lin(T.oln[:], ln, 0.5, T.nb[:, 0:1], ["ln", "nb"], ["oln"])
-            dma("y", T.ol[:, C:2 * C], T.oln[:], ["oln"], [])
-            lin(T.mg[:], T.lr[:].indirect(T.offm[:]), -1.0, 1.0, flags + ["offm", "lr"], ["mg"])
-        scan(T.e1[:], T.d0[:], win[:, 0:288], -4096.0, A.add, A.max, ["d0a", "d0b", ak], ["e1"])
-        tr(T.n2t[:], T.n2[:], ["n2"], ["n2t"])
-        scan(T.e2[:], T.pen[:], T.e1[:, 1:288:2], 0.0, A.add, A.min, ["pen", "e1"], ["e2"])
-        ts(T.offn[:], T.n2t[:].indirect(T.offf[:]), float(CAP), A.min, ["n2t", "offf"], ["offn"])
-        ts(T.offp[:], T.e2[:, 3:CAP:4], 1024.0, A.min, ["e2", "pc8"], ["offp"], pc[8], A.add)
+        flags = ["ll%d" % d for d in range(1, 6)] + ["rr%d" % d for d in range(6)]
         fk = ["f0", "f1", "f2", "f3", "fz", "offp"]
-        cp(T.pt[:, 0:288], T.fp[:, 0:4 * C + 4].indirect(T.offp[:, 0:18]), fk, ["p0"])
-        act(T.pt[:, 288:576], T.fp[:, 0:4 * C + 4].indirect(T.offp[:, 18:36]), fk, ["p1"])
+
+        def numbered(kind, d):
+            if kind == "f":
+                act(T.fp[:, d:4 * C:4], bank(T.psf, d, C), ["Bf%d" % d], ["f%d" % d])
+            elif kind == "g":
+                e = slice(128 * d, 128 * d + 128)
+                mm(bank(T.psf, d, 128), T.qe[:, e], T.se[:, e], q[:, 0:128], s[:, 0:128], qk, ["Bf%d" % d], False)
+            elif kind == "w":
+                a, k = {2: (1, 1), 3: (2, 2), 4: (2, 2), 5: (4, 4)}[d]
+                lo = 32 if d == 3 else 27
+                tt(W(d, lo, 70 - d), W(a, lo, 70 - d), W(d - k, lo + k, 70 - d + k), A.min, ["w%d" % a, "w%d" % (d - k)], ["w%d" % d])
+            elif kind == "l":
+                n, k = (37, 5) if d == 5 else (32, 1)
+                tt(T.lr[:, 6 - d:6 * n:6], W(1, 32, 32 + n), W(k, 32 - d, 32 + n - d), A.is_lt, ["w1", "w%d" % k, "lr"], ["ll%d" % d])
+            elif kind == "r":
+                o = 1 if d == 5 else 0
+                n = 37 - d if last else 32
+                tt(T.lr[:, R0 + 6 + d - 6 * o:R0 + 6 + 6 * n:6], W(1, 32 - o, 32 + n), W(d, 33 - o, 33 + n), A.is_le,
+                   ["w1", "w%d" % d, "lr"], ["rr%d" % d])
+            elif t == 0 and d == 1:
+                ts(T.eo[:, 3:515:4], T.jj[:], 1024.0, A.add, ["jj", "eo", "pc14"], ["eo"], pc[14], A.is_equal)
+            elif t == 0:
+                ts(T.offe[:, 0:1], T.pf[:, 9:10], 16.0, A.add, ["pf9"], ["offe"])
+
+        def counts_out():
+            if last:
+                lin(T.oln[:], T.ln[:], 0.5, T.nb[:, 0:1], ["ln", "nb"], ["oln"])
+                dma("y", T.ol[:, C:2 * C], T.oln[:], ["oln"], [])
+
+        steps = {
+            "gt": lambda: tt(T.gt[:, 0:5], T.ww[:, 32:417:96], T.ww[:, 421:32:-97], A.is_gt, ["w1", "w2", "w3", "w4", "w5"], ["gt"]),
+            "ch": lambda: tt(T.ch[:], T.lr[:, R0 + 5:R0 + 197:6], T.lr[:, 31:222:6], A.max, ["rr5", "ll5"], ["ch"]),
+            "hh": lambda: scan(T.hh[:, 6:198], T.lr[:, 0:192], T.lr[:, R0 + 6:R0 + 198], 0.0, A.mult, A.max, flags, ["hh"]),
+            "ln": lambda: scan(T.ln[:], T.ch[:], T.ch[:], pc[4], A.add, A.add, ["ch", "pc4"], ["ln"]),
+            "yy": lambda: scan(T.pd[:, 1:64:2], T.hh[:, 5:197:6], T.hh[:, 11:198:6], T.ln[:, 0:1], A.add, A.add,
+                               ["hh", "hh0", "ln"], ["yy"]),
+            "dl": lambda: scan(T.dl[:, 0:6], T.hh[:, 35:4:-6], T.gt[:, 0:6], 0.0, A.add, A.mult, ["hh", "hh0", "gt", "gt5"], ["dl"]),
+            "or": lambda: tt(T.pm[:, 1:64:4], T.hh[:, 11:200:12], T.hh[:, 17:204:12], A.max, ["hh", "pm"], ["or"]),
+            "ob": lambda: ts(T.offb[:, 0:1], T.ln[:, 31:32], 0.5, A.mult, ["ln", "pc9"], ["offb"], pc[9], A.add),
+            "pl": lambda: scan(T.pl[:], T.pm[:], T.pd[:], 0.0, A.mult, A.add, ["or", "yy", "pm", "pm2", "pd0", "pd2"], ["pl"]),
+            "bs": lambda: before(T.base[:, 0:1], T.j0[:], 2.0, pc[7], tabs + ["offb", "pc7"], ["base"]),
+            "nb": lambda: before(T.nb[:, 0:1], T.j1[:], 1.0, pc[6], tabs + ["offb", "pc6"], ["nb"]),
+            "of": lambda: ts(T.offs[:], T.pl[:, 2:64:4], T.base[:, 0:1], A.add, ["pl", "base", "dl"], ["offs"], T.dl[:, 5:6], A.subtract),
+            "sc": lambda: cp(win[:].indirect(T.offs[:]), T.vc[:], ["offs", "vc"], [ak]),
+            "n2": lambda: lin(T.n2[:], T.ln[:].indirect(T.offr[:]), 0.5, T.nb[:, 0:1], ["ln", "offr", "nb"], ["n2"]),
+            "ol": counts_out,
+            "e1": lambda: scan(T.e1[:], T.d0[:], win[:, 0:288], -4096.0, A.add, A.max, ["d0a", "d0b", ak], ["e1"]),
+            "nt": lambda: tr(T.n2t[:], T.n2[:], ["n2"], ["n2t"]),
+            "e2": lambda: scan(T.e2[:], T.pen[:], T.e1[:, 1:288:2], 0.0, A.add, A.min, ["pen", "e1"], ["e2"]),
+            "on": lambda: ts(T.offn[:], T.n2t[:].indirect(T.offf[:]), float(CAP), A.min, ["n2t", "offf"], ["offn"]),
+            "oa": lambda: ts(T.offa[:], T.n2t[:].indirect(T.offf[:, 0:1]), pc[15], A.max, ["n2t", "offf", "pc15"], ["offa"],
+                             float(CAP), A.min),
+            "oo": lambda: ts(T.offo[:], T.n2t[:].indirect(T.offe[:, 0:1]), float(CAP), A.min, ["n2t", "offe"], ["offo"]),
+            "op": lambda: ts(T.offp[:], T.e2[:, 3:CAP:4], 1024.0, A.min, ["e2", "pc8"], ["offp"], pc[8], A.add),
+            "pv": lambda: cp(T.pt[:, 0:16 * PV], T.fp[:, 0:4 * C + 4].indirect(T.offp[:, 0:PV]), fk, ["p0"]),
+            "ps": lambda: act(T.pt[:, 16 * PV:576], T.fp[:, 0:4 * C + 4].indirect(T.offp[:, PV:36]), fk, ["p1"]),
+        }
+        for word in LISTS.split():
+            if word in steps:
+                steps[word]()
+            else:
+                numbered(word[0], int(word[1]))
         quant(T.qp[:], T.sp[:], T.pt[:], ["p0", "p1"], ["qp"])
         lq, lp = [(T.lq0, T.lp0), (T.lq1, T.lp1)][t]
         for b in (2, 0, 3, 1):
             e = slice(128 * b, 128 * b + 128)
             mm(bank(T.psr, b, CAP), lq[:, e], lp[:, e], T.qp[:], T.sp[:], ["qp", "lq%d" % t, "lp%d" % t], ["Br%d" % b])
         if last:
-            scan(T.mk[:], T.md[:], T.mg[:], 0.0, A.add, A.mult, ["mg", "md"], ["mk"])
-        else:
+            lin(T.mg[:], T.lr[:].indirect(T.offm[:]), -1.0, 1.0, flags + ["offm", "lr"], ["mg"])
             quant(T.qv[:], T.sv[:], T.vt[:], ["vt"], ["qv"])
+        else:
+            for b in range(4):
+                quant(T.qo[:, 128 * b:128 * b + 128], T.so[:, 128 * b:128 * b + 128], T.eo[:, 3 - b:515 - b], ["eo"], ["qo%d" % b])
+            lin(T.a1[:, 0:288], T.tab[:, 0:288], 0.0, -2048.0, tabs, ["a1"])
+            lin(T.md[:], T.tab[:, 0:256], 0.0, 1.0, tabs, ["md"])
         for b in (2, 0, 3, 1):
             if b < 2:
                 ts(T.ht[:, b:4 * CAP:4], bank(T.psr, b, CAP), 0.03125, A.mult, ["Br%d" % b], ["h%d" % b])
             else:
                 act(T.ht[:, b:4 * CAP:4], bank(T.psr, b, CAP), ["Br%d" % b], ["h%d" % b], 0.03125)
-        quant(T.qh[:], T.sh[:], T.ht[:], ["h0", "h1", "h2", "h3"], ["qh"])
-        for b in range(4):
-            e = slice(128 * b, 128 * b + 128)
-            mm(bank(T.psr, b, CAP), T.qe[:, e], T.se[:, e], T.qh[:], T.sh[:], ["qh", "qe%d" % b], ["Br%d" % b])
         if last:
+            scan(T.mk[:], T.md[:], T.mg[:], 0.0, A.add, A.mult, ["mg", "md"], ["mk"])
             lin(T.olm[:], T.mk[:, 7:256:8], 1.0, pc[0], ["mk", "pc0"], ["olm"])
             dma("y", T.ol[:, 0:C], T.olm[:], ["olm"], [])
+        else:
+            act(T.md[:, 7:256:8], T.jj[:, 0:32], ["jj"], ["md"])
+        quant(T.qh[:], T.sh[:], T.ht[:, 0:584], ["h0", "h1", "h2", "h3", "hz"], ["qh"])
+        picked = {"A": (T["pa%d" % t], T["sa%d" % t], T.offa[:, 0:8], "offa"),
+                  "B": (T["pb%d" % t], T["sb%d" % t], T.offo[:, 0:8], "offo")}
 
         new = tiles[t + 1]
         for word in PLAN[t].split():
             kind = word[0]
-            if kind == "q":
+            if kind == "m":
+                b = int(word[1])
+                e = slice(128 * b, 128 * b + 128)
+                mm(bank(T.psr, b, CAP), T.qe[:, e], T.se[:, e], T.qh[:, 0:CAP], T.sh[:, 0:CAP], ["qh", "qe%d" % b], ["Br%d" % b])
+            elif kind == "P":
+                pq, ps, off, ok = picked[word[1]]
+                cp(pq[:].bitcast(dt.uint32), T.qh[:].bitcast(dt.uint32).indirect(off), ["qh", ok], [word])
+            elif kind == "S":
+                pq, ps, off, ok = picked[word[1]]
+                if word[2] == "v":
+                    cp(ps[:], T.sh[:].indirect(off), ["qh", ok], [word[:2]])
+                else:
+                    op("s", lambda: S.activation(ps[:], T.sh[:].indirect(off), ACT.Copy), ["qh", ok], [word[:2]])
+            elif kind == "E":
+                b = int(word[1])
+                e = slice(128 * b, 128 * b + 128)
+
+                def both():
+                    out = bank(T.psf, b, 128)
+                    g.tensor.matmul_mx(out, T.qe[:, e], T.se[:, e], picked["A"][0][:], picked["A"][1][:], False, False)
+                    return g.tensor.matmul_mx(out, T.qo[:, e], T.so[:, e], picked["B"][0][:], picked["B"][1][:], False, True)
+
+                op("p", both, ["PA", "PB", "SA", "SB", "qo%d" % b], ["Bf%d" % b], adds=True)
+            elif kind == "k":
+                b = int(word[1])
+                (cp if word[2] == "v" else act)(new[:, b:512:4], bank(T.psf, b, 128), ["Bf%d" % b], ["T%d0" % b])
+            elif kind == "q":
                 quant_piece(t + 1, word[1:])
             elif kind == "t":
                 turn(word[1:])
-            elif kind == "c":
-                a, z = span(word[1:])
-                dma("y", T.oc[:, 4 * a:4 * z], T.q2[:, a:z].bitcast(dt.uint8), ["q2" + k for k in word[1:]], [])
-            elif kind == "y":
+            elif kind == "o":
+                k = int(word[1])
+                dma(word[2], T.osc[4 * k:4 * k + 4, :], T.s2[32 * k:32 * k + 4, :], ["q20", "q21", "q22", "q23"], [])
+            elif kind in "cyz":
                 w = word[1:-1]
                 a, z = span(w)
-                if w[-1] == "3":
-                    for k in range(4):
-                        dma("ys"[k % 2], T.osc[4 * k:4 * k + 4, :], T.s2[32 * k:32 * k + 4, :], ["q20", "q21", "q22", "q23"], [])
-                (cp if word[-1] == "v" else act)(T.ysb[:, a:z], bank(T.psr, int(w[0]), z - a), ["Br" + w[0]], ["y" + w])
-                dma("s" if w[-1] == "3" else "y", T.y[:, a:z], T.ysb[:, a:z], ["y" + w], [])
+                if kind == "c":
+                    dma(word[-1], T.oc[:, 4 * a:4 * z], T.q2[:, a:z].bitcast(dt.uint8), ["q2" + k for k in w], [])
+                elif kind == "z":
+                    dma(word[-1], T.y[:, a:z], T.ysb[:, a:z], ["y" + k for k in w], [])
+                else:
+                    (cp if word[-1] == "v" else act)(T.ysb[:, a:z], bank(T.psr, int(w[0]), z - a), ["Br" + w[0]], ["y" + k for k in w])
             elif kind == "h":
                 b = int(word[1])
                 (cp if word[2] == "v" else act)(T.dh[:, DW * b:DW * b + CAP], bank(T.psr, b, CAP), ["Br%d" % b], ["dh%d" % b])

@@ -16,7 +16,7 @@ for _d, _l in (
          "sa0 128 sb0 128 sa1 128 sb1 128"),
     (I32, "pi 12"),
     (U16, "offg 12 offr 4 offf 2 offs 16 offp 36 offn 32 offb 2 offm 16 offa 16 offo 16 offe 2"),
-    (F32, "ysb 512 olm 32 oln 32 jj 128 pf 12 pc 16 r4 144 ct 16 p4 4 tab 544 xs 576 zz 96 ww 480 "
+    (F32, "ysb 512 olm 32 oln 32 jj 128 pf 12 pc 16 r4 144 ct 16 p4 4 tab 544 xs 576 zz 96 ww 480 rs 48 fw 72 bw 72 "
           "pd 64 pm 64 pl 64 ch 32 ln 32 gt 8 dl 8 base 2 nb 2 j0 16 j1 16 n2 64 n2t 64"),
 ):
     _w = _l.split()
@@ -24,11 +24,11 @@ for _d, _l in (
         SCRATCH[_w[_i]] = ("sbuf", [128, int(_w[_i + 1])], _d)
 SEMAPHORES = ["cv", "cs", "cp", "cg", "sent", "ap0", "aq0", "ap1", "aq1", "stored"] + ["d%d" % i for i in range(10)]
 
-LISTS = ("f0 f1 c2 w2 l1 r1 l2 w4 w3 l3 r2 w5 l4 r4 r3 l5 r5 gt ch hh ln or ob bs nb n2 f2 f3 g0 g1 g2 g3 yy dl c1 pl of "
-         "sc ol e1 nt e2 on op oa pv ps oo")
+LISTS = ("f0 f1 fw bw w2 l3 l2 l4 w5 w3 w4 l1 r2 l5 r5 r4 r1 r3 ch gt hh ln or ob bs nb n2 f2 f3 g0 g1 g2 g3 yy dl pl c1 "
+         "of c2 sc ol e1 nt e2 on op oa pv ps oo")
 PLAN = [
-    "PA m1 SBs m2 m0 PB m3 h1s SAs E3 h2v h3s f21 d1123 h0s d323 d023 f223 E2 a21 E0 f01 a223 k3s f31 a01 a31 E1 k1s "
-    "k2s q2 q3 k0s q1 q0 t2 t3 t1 t0",
+    "SAs PA m2 h2s m0 m1 SBs PB m3 h0v E3 d2123 h1s h3s d1123 E0 f0123 f323 d31 a01 E2 a023 k3s E1 a32 k1s a33 k2s q1 "
+    "q2 q3 k0s q0 t1 t2 t3 t0",
     "m2 SAs SBs m0 m3 PA h2v PB d2123 m1 E3 h0s h3s E1 h1s f31 E0 E2 d01 a31 f11 f023 k3s a11 d32 k0s q1 k1s c1y k2s "
     "f33 d123 q0 a02 a33 a03 c0y y1s q2 z1y q3 y0v c2s c3s o1y y2v o2s z0s o0y z2y y3v z3y o3s",
 ]
@@ -188,18 +188,20 @@ def rank_program(g, core, T, topo):
         quant(T.qe[:, 128 * b:128 * b + 128], T.se[:, 128 * b:128 * b + 128], T.eb[:, 3 - b:515 - b], ["eb"], ["qe%d" % b])
     quant(T.qu[:], T.su[:], T.ut[:], ["ut"], ["qu"])
 
+    lin(T.rs[:, 0:45], T.jj[:, 0:45], 0.0, -9 * BIG, ["jj"], ["rs"])
     for k in range(0, 544, 128):
         n = min(128, 544 - k)
         lin(T.tab[:, k:k + n], T.jj[:, 0:n], 1.0, float(k), ["jj"], ["tab%d" % k])
     tabs = ["tab%d" % k for k in range(0, 544, 128)]
+    lin(T.rs[:, 0:45:5], T.jj[:, 0:9], 0.0, 9 * BIG, ["jj"], ["rs"])
     lin(pc[0], piece, 32.0, 0.0, ["pf"], ["pc0"])
     lin(pc[2], odd, 31.5, half, ["pf"], ["pc2"])
     lin(pc[12], lane, -1.0, piece, ["pf"], ["pc12"])
     lin(pc[10], step, -5.75, pc[3], ["pf", "pc3"], ["pc10"])
     lin(pc[5], piece, -34.0, 511.0, ["pf"], ["pc5"])
-    act(T.lr[:], T.tab[:, 0:464], tabs, ["lr"], 0.0)
     act(T.pm[:], T.jj[:, 0:64], ["jj"], ["pm"], 0.0)
     lin(pc[13], piece, 0.5, pc[2], ["pf", "pc2"], ["pc13"])
+    act(T.lr[:], T.tab[:, 0:464], tabs, ["lr"], 0.0)
     lin(pc[11], piece, 0.75, pc[10], ["pf", "pc10"], ["pc11"])
     lin(pc[4], pc[1], -34.0, -2.0, ["pc1"], ["pc4"])
     lin(pc[6], piece, 34.0, -544.0, ["pf"], ["pc6"])
@@ -246,10 +248,10 @@ def rank_program(g, core, T, topo):
     for t in range(ROUNDS):
         ts(T.offg[:, 6 * t:6 * t + 6], T.jj[:, 0:96:16], pc[0], A.add, ["jj", "pc0"], ["offg%d" % t], float(t), A.add)
     quant_piece(0, "2")
-    turn("01")
     ts(T.offf[:], T.jj[:, 0:16:8], pc[13], A.add, ["jj", "pc13"], ["offf"])
     ts(T.offr[:], T.p4[:], piece, A.add, ["p4", "pf"], ["offr"])
     quant_piece(0, "3")
+    turn("01")
     turn("2")
     ts(T.pen[:], T.r4[:], pc[12], A.is_le, ["r4", "pc12"], ["pen"], 4096.0, A.mult)
     turn("3")
@@ -278,10 +280,11 @@ def rank_program(g, core, T, topo):
             elif kind == "g":
                 e = slice(128 * d, 128 * d + 128)
                 mm(bank(T.psf, d, 128), T.qe[:, e], T.se[:, e], q[:, 0:128], s[:, 0:128], qk, ["Bf%d" % d], False)
+            elif kind == "w" and d == 5:
+                tt(W(5, 27, 65), T.bw[:, 27:65], T.fw[:, 31:69], A.min, ["fw", "bw"], ["w5"])
             elif kind == "w":
-                a, k = {2: (1, 1), 3: (2, 2), 4: (2, 2), 5: (4, 4)}[d]
-                lo = 32 if d == 3 else 27
-                tt(W(d, lo, 70 - d), W(a, lo, 70 - d), W(d - k, lo + k, 70 - d + k), A.min, ["w%d" % a, "w%d" % (d - k)], ["w%d" % d])
+                a, k = {2: (1, 1), 3: (2, 2), 4: (2, 2)}[d]
+                tt(W(d, 32, 70 - d), W(a, 32, 70 - d), W(d - k, 32 + k, 70 - d + k), A.min, ["w%d" % a, "w%d" % (d - k)], ["w%d" % d])
             elif kind == "l":
                 n, k = (37, 5) if d == 5 else (32, 1)
                 tt(T.lr[:, 6 - d:6 * n:6], W(1, 32, 32 + n), W(k, 32 - d, 32 + n - d), A.is_lt, ["w1", "w%d" % k, "lr"], ["ll%d" % d])
@@ -301,6 +304,8 @@ def rank_program(g, core, T, topo):
                 dma("y", T.ol[:, C:2 * C], T.oln[:], ["oln"], [])
 
         steps = {
+            "fw": lambda: scan(T.fw[:, 27:72], T.rs[:, 0:45], W(1, 27, 72), 0.0, A.max, A.min, ["w1", "rs"], ["fw"]),
+            "bw": lambda: scan(T.bw[:, 71:26:-1], T.rs[:, 0:45], T.ww[:, 455:410:-1], 0.0, A.max, A.min, ["w1", "rs"], ["bw"]),
             "gt": lambda: tt(T.gt[:, 0:5], T.ww[:, 32:417:96], T.ww[:, 421:32:-97], A.is_gt, ["w1", "w2", "w3", "w4", "w5"], ["gt"]),
             "ch": lambda: tt(T.ch[:], T.lr[:, R0 + 5:R0 + 197:6], T.lr[:, 31:222:6], A.max, ["rr5", "ll5"], ["ch"]),
             "hh": lambda: scan(T.hh[:, 6:198], T.lr[:, 0:192], T.lr[:, R0 + 6:R0 + 198], 0.0, A.mult, A.max, flags, ["hh"]),

from concourse.mybir import dt, AluOpType, ActivationFunctionType

C, CAP, ROUNDS = 512, 144, 2
BIG = 1.0e29
DW = 160
R0 = 224
PV = 18
F32, BF, U16, I32, X4, U8 = "float32", "bfloat16", "uint16", "int32", "float8_e4m3fn_x4", "uint8"
SCRATCH = {"psf": ("psum", [128, 2048], F32), "psr": ("psum", [128, 2048], F32)}
for _d, _l in (
    (BF, "xt 2048 ut 512 vt 512 t1 2048 t2 2048 eb 520 eo 520 fp 2064 dh 640 gb 2048 pt 576 ht 592 lr 464 hh 208 "
         "a0 4128 a1 4128 vc 256 d0 288 e1 288 e2 144 pen 144 mg 256 md 256 mk 256"),
    (X4, "q0 512 q1 512 q2 512 qu 128 qv 128 wq 512 lq0 512 lq1 512 qe 512 qo 512 qp 144 qh 146 "
         "pa0 128 pb0 128 pa1 128 pb1 128"),
    (U8, "s0 512 s1 512 s2 512 su 128 sv 128 wp 512 lp0 512 lp1 512 se 512 so 512 sp 144 sh 146 "
         "sa0 128 sb0 128 sa1 128 sb1 128"),
    (I32, "pi 12"),
    (U16, "offg 12 offr 4 offf 2 offs 16 offp 36 offn 32 offb 2 offm 16 offa 16 offo 16 offe 2"),
    (F32, "ysb 512 olm 32 oln 32 jj 128 pf 12 pc 16 r4 144 ct 16 p4 4 tab 544 xs 576 zz 96 ww 480 rs 48 fw 72 bw 72 "
          "pd 64 pm 64 pl 64 ch 32 ln 32 gt 8 dl 8 base 2 nb 2 j0 16 j1 16 n2 64 n2t 64"),
):
    _w = _l.split()
    for _i in range(0, len(_w), 2):
        SCRATCH[_w[_i]] = ("sbuf", [128, int(_w[_i + 1])], _d)
SEMAPHORES = ["cv", "cs", "cp", "cg", "sent", "ap0", "aq0", "ap1", "aq1", "stored"] + ["d%d" % i for i in range(10)]

LISTS = ("f0 f1 fw bw w2 l3 l2 l4 w5 w3 w4 l1 r2 l5 r5 r4 r1 r3 ch gt hh ln or ob bs nb n2 f2 f3 g0 g1 g2 g3 yy dl pl c1 "
         "of c2 sc ol e1 nt e2 on op oa pv ps oo")
PLAN = [
    "SAs PA m2 h2s m0 m1 SBs PB m3 h0v E3 d2123 h1s h3s d1123 E0 f0123 f323 d31 a01 E2 a023 k3s E1 a32 k1s a33 k2s q1 "
    "q2 q3 k0s q0 t1 t2 t3 t0",
    "m2 SAs SBs m0 m3 PA h2v PB d2123 m1 E3 h0s h3s E1 h1s f31 E0 E2 d01 a31 f11 f023 k3s a11 d32 k0s q1 k1s c1y k2s "
    "f33 d123 q0 a02 a33 a03 c0y y1s q2 z1y q3 y0v c2s c3s o1y y2v o2s z0s o0y z2y y3v z3y o3s",
]


def rank_program(g, core, T, topo):
    rank = T.rank_of(core)
    if rank is None:
        return
    A, ACT = AluOpType, ActivationFunctionType
    n_ranks = len(T.cores)
    Q = {"v": g.vector, "s": g.scalar, "p": g.tensor, "g": g, "y": g.sync}
    V, S = g.vector, g.scalar
    count = {"cv": 0, "cs": 0, "cp": 0, "cg": 0, "stored": 0}
    known = {e: {} for e in Q}
    waited = {}
    wrote, read = {}, {}
    loads = []

    def need(e, marks):
        for m in sorted(marks, key=lambda k: -k[1]):
            sem, val, clock = m[0], m[1], m[2]
            if known[e].get(sem, 0) < val:
                Q[e].wait_ge(T.sem[sem], val)
                waited[sem] = max(waited.get(sem, 0), val)
                known[e][sem] = val
                for k, x in clock.items():
                    if known[e].get(k, 0) < x:
                        known[e][k] = x

    def op(e, call, r=(), w=(), dma=False, adds=False):
        marks = []
        for k in r:
            marks.append(wrote[k])
            if k[0] == "B":
                marks += [m for m in read.get(k, []) if m[3] != e]
        for k in w:
            if k in wrote and not adds:
                marks.append(wrote[k])
            marks += read.get(k, [])
        need(e, marks)
        if dma and not w:
            call().then_inc(T.sem.stored, 16)
            count["stored"] += 16
            return
        if dma:
            sem = "d%d" % len(loads)
            call().then_inc(T.sem[sem], 16)
            me = (sem, 16, dict(known[e]), "dma")
            loads.append(me)
        else:
            sem = "c" + e
            call().then_inc(T.sem[sem], 1)
            count[sem] += 1
            me = (sem, count[sem], dict(known[e]), e)
        for k in r:
            read.setdefault(k, []).append(me)
        for k in w:
            wrote[k] = me
            read[k] = []

    def tt(out, a, b, o, r, w):
        op("v", lambda: V.tensor_tensor(out, a, b, o), r, w)

    def ts(out, a, s1, o1, r, w, s2=None, o2=None):
        if s2 is None:
            op("v", lambda: V.tensor_scalar(out, a, s1, None, o1), r, w)
        else:
            op("v", lambda: V.tensor_scalar(out, a, s1, s2, o1, o2), r, w)

    def cp(out, a, r, w):
        op("v", lambda: V.tensor_copy(out, a), r, w)

    def fill(out, c, w):
        op("v", lambda: V.memset(out, c), (), w)

    def tr(out, a, r, w):
        op("v", lambda: V.transpose(out, a), r, w)

    def scan(out, a, b, init, o0, o1, r, w):
        op("v", lambda: V.tensor_tensor_scan(out, a, b, init, o0, o1), r, w)

    def act(out, a, r, w, scale=1.0):
        op("s", lambda: S.activation(out, a, ACT.Copy, scale=scale), r, w)

    def lin(out, a, scale, bias, r, w):
        op("s", lambda: S.activation(out, a, ACT.Identity, bias=bias, scale=scale), r, w)

    def before(out, junk, scale, bias, r, w):
        op("s", lambda: S.activation(junk, T.tab[:].indirect(T.offb[:, 0:1]), ACT.Relu, bias=bias, scale=scale, accum_out=out), r, w)

    def quant(q, s, a, r, w):
        op("v", lambda: V.quantize_mx(q, s, a), r, w)

    def mm(out, lq, ls, rq, rs, r, w, stop=True):
        op("p", lambda: g.tensor.matmul_mx(out, lq, ls, rq, rs, True, stop), r, w)

    def iota(out, pattern, base, cm, w, flag=True):
        if flag:
            op("g", lambda: g.iota(out, pattern, base, cm, allow_small_or_imprecise_dtypes=True), (), w)
        else:
            op("g", lambda: g.iota(out, pattern, base, cm), (), w)

    def dma(e, out, a, r, w):
        op(e, lambda: Q[e].dma_start(out, a), r, w, dma=True)

    def bank(buf, b, n, first=0):
        return buf[:, 512 * b + first:512 * b + first + n]

    dma("y", T.xt[:, 0:1024], T.x[:, 0:1024], (), ["x0", "x1"])
    dma("s", T.ut[:], T.u[:], (), ["ut"])
    dma("s", T.xt[:, 1024:1536], T.x[:, 1024:1536], (), ["x2"])
    dma("y", T.xt[:, 1536:2048], T.x[:, 1536:2048], (), ["x3"])
    dma("s", T.wp[:], T.ws[:], (), ["wp"])
    dma("y", T.wq[:].bitcast(dt.uint8), T.wc[:], (), ["wq"])
    dma("y", T.vt[:], T.v[:], (), ["vt"])

    sent = [0]

    def send(dst_ap, src_ap, sem, t, key):
        peer = T.cores[(rank - 1 - t) % n_ranks]
        rid, pid, _ = topo.addr(peer)
        need("g", [wrote[key]])
        g.remote_dma(dst_ap, src_ap, T.sem[sem], T.sem.sent, pid, rid, topo.mask(core, peer))
        sent[0] += len(topo.engines(core, peer))

    for t in range(ROUNDS):
        k = len(topo.engines(T.cores[(rank + 1 + t) % n_ranks], core))
        wrote["lp%d" % t] = ("ap%d" % t, k, {}, "far")
        wrote["lq%d" % t] = ("aq%d" % t, k, {}, "far")

    iota(T.pi[:, 8:9], [[0, 1]], 0, 1, ["pi8"], flag=False)
    iota(T.jj[:], [[1, 128]], 0, 0, ["jj"])
    iota(T.p4[:], [[16, 2], [0, 2]], 0, 0, ["p4"])
    iota(T.ct[:], [[1, 16]], 1032, 16, ["ct"])
    iota(T.r4[:], [[0, CAP // 4], [4, 4]], 0, 0, ["r4"])
    iota(T.vc[:], [[8, 16], [128, 16]], -1024, 0, ["vc"])
    send(T.lp0[:], T.wp[:], "ap0", 0, "wp")
    send(T.lq0[:].bitcast(dt.uint8), T.wq[:].bitcast(dt.uint8), "aq0", 0, "wq")
    send(T.lp1[:], T.wp[:], "ap1", 1, "wp")
    send(T.lq1[:].bitcast(dt.uint8), T.wq[:].bitcast(dt.uint8), "aq1", 1, "wq")

    fill(T.eb[:], 0.0, ["eb"])
    p = T.pi[:, 8:9]
    for k, bits in enumerate((15, 16, 1, 3, 7)):
        ts(T.pi[:, k:k + 1], p, bits, A.bitwise_and, ["pi8"], ["pi%d" % k])
    fill(T.xs[:, 0:32], -BIG, ["xsl"])
    cp(T.pf[:, 8:9], p, ["pi8"], ["pf8"])
    cp(T.pf[:, 0:5], T.pi[:, 0:5], ["pi%d" % k for k in range(5)], ["pf"])
    piece, half, odd, lane, step = [T.pf[:, i:i + 1] for i in range(5)]
    fill(T.xs[:, 544:576], BIG, ["xsr"])
    ts(T.eb[:, 3:515:4], T.jj[:], T.pf[:, 8:9], A.is_equal, ["jj", "pf8", "eb"], ["eb"])
    pc = [T.pc[:, i:i + 1] for i in range(16)]
    ts(pc[1], piece, -1.0, A.add, ["pf"], ["pc1"], piece, A.mult)
    ts(pc[3], step, 7.0, A.is_equal, ["pf"], ["pc3"], -float(R0 + 6), A.mult)
    for b in range(4):
        quant(T.qe[:, 128 * b:128 * b + 128], T.se[:, 128 * b:128 * b + 128], T.eb[:, 3 - b:515 - b], ["eb"], ["qe%d" % b])
    quant(T.qu[:], T.su[:], T.ut[:], ["ut"], ["qu"])

    lin(T.rs[:, 0:45], T.jj[:, 0:45], 0.0, -9 * BIG, ["jj"], ["rs"])
    for k in range(0, 544, 128):
        n = min(128, 544 - k)
        lin(T.tab[:, k:k + n], T.jj[:, 0:n], 1.0, float(k), ["jj"], ["tab%d" % k])
    tabs = ["tab%d" % k for k in range(0, 544, 128)]
    lin(T.rs[:, 0:45:5], T.jj[:, 0:9], 0.0, 9 * BIG, ["jj"], ["rs"])
    lin(pc[0], piece, 32.0, 0.0, ["pf"], ["pc0"])
    lin(pc[2], odd, 31.5, half, ["pf"], ["pc2"])
    lin(pc[12], lane, -1.0, piece, ["pf"], ["pc12"])
    lin(pc[10], step, -5.75, pc[3], ["pf", "pc3"], ["pc10"])
    lin(pc[5], piece, -34.0, 511.0, ["pf"], ["pc5"])
    act(T.pm[:], T.jj[:, 0:64], ["jj"], ["pm"], 0.0)
    lin(pc[13], piece, 0.5, pc[2], ["pf", "pc2"], ["pc13"])
    act(T.lr[:], T.tab[:, 0:464], tabs, ["lr"], 0.0)
    lin(pc[11], piece, 0.75, pc[10], ["pf", "pc10"], ["pc11"])
    lin(pc[4], pc[1], -34.0, -2.0, ["pc1"], ["pc4"])
    lin(pc[6], piece, 34.0, -544.0, ["pf"], ["pc6"])
    lin(pc[7], piece, 68.0, -1088.0, ["pf"], ["pc7"])
    lin(pc[8], lane, 1.0, 1024.0, ["pf"], ["pc8"])
    lin(pc[9], pc[1], 17.0, pc[5], ["pc1", "pc5"], ["pc9"])
    lin(T.pf[:, 9:10], half, -1.0, pc[13], ["pf", "pc13"], ["pf9"])
    lin(T.lr[:, R0 + 6:R0 + 223:6], T.jj[:, 0:37], 0.0, 1.0, ["jj", "lr"], ["rr0"])
    act(T.hh[:, 5:6], T.jj[:, 0:1], ["jj"], ["hh0"], 0.0)
    lin(T.gt[:, 5:6], T.jj[:, 0:1], 0.0, 2.0, ["jj"], ["gt5"])
    act(T.pd[:, 0:64:4], T.ct[:], ["ct"], ["pd0"], -1.0)
    act(T.pd[:, 2:64:4], T.ct[:], ["ct"], ["pd2"])
    lin(T.pm[:, 2:64:4], T.ct[:], 0.0, 1.0, ["ct", "pm"], ["pm2"])
    act(T.fp[:, 4 * C:4 * C + 4], T.jj[:, 0:4], ["jj"], ["fz"], 0.0)
    act(T.dh[:, CAP:4 * DW:DW], T.jj[:, 0:4], ["jj"], ["dz"], 0.0)
    act(T.ht[:, 576:584], T.jj[:, 0:8], ["jj"], ["hz"], 0.0)
    lin(pc[14], half, 64.0, T.pf[:, 8:9], ["pf", "pf8"], ["pc14"])
    lin(pc[15], half, 9.0, 0.0, ["pf"], ["pc15"])
    act(T.d0[:, 0:288:2], T.r4[:], ["r4"], ["d0a"], 0.0)
    lin(T.d0[:, 1:288:2], T.r4[:], 0.0, 4.0, ["r4"], ["d0b"])
    lin(T.a0[:, 0:288], T.tab[:, 0:288], 0.0, -2048.0, tabs, ["a0"])
    act(T.eo[:], T.tab[:, 0:520], tabs, ["eo"], 0.0)

    tiles = [T.xt, T.t1, T.t2]
    codes = [(T.q0, T.s0), (T.q1, T.s1), (T.q2, T.s2)]

    def span(w):
        return 128 * int(w[0]), 128 * int(w[-1]) + 128

    def quant_piece(t, w):
        q, s = codes[t]
        a, b = span(w)
        keys = ["x" + k for k in w] if t == 0 else ["T%d%s" % (j, k) for j in range(4) for k in w]
        done = ["q%d%s" % (t, k) for k in w]
        quant(q[:, a:b], s[:, a:b], tiles[t][:, 4 * a:4 * b], keys, done)
        side = (T.qu[:], T.su[:], "qu") if t < ROUNDS else (T.qv[:], T.sv[:], "qv")
        mm(bank(T.psr, int(w[0]), b - a), side[0], side[1], q[:, a:b], s[:, a:b], [side[2]] + done, ["Br" + w[0]])

    def turn(w):
        a, b = span(w)
        tr(T.xs[:, 32 + a:32 + b], bank(T.psr, int(w[0]), b - a), ["Br" + w[0]], ["xs" + k for k in w])

    quant_piece(0, "01")
    for t in range(ROUNDS):
        ts(T.offg[:, 6 * t:6 * t + 6], T.jj[:, 0:96:16], pc[0], A.add, ["jj", "pc0"], ["offg%d" % t], float(t), A.add)
    quant_piece(0, "2")
    ts(T.offf[:], T.jj[:, 0:16:8], pc[13], A.add, ["jj", "pc13"], ["offf"])
    ts(T.offr[:], T.p4[:], piece, A.add, ["p4", "pf"], ["offr"])
    quant_piece(0, "3")
    turn("01")
    turn("2")
    ts(T.pen[:], T.r4[:], pc[12], A.is_le, ["r4", "pc12"], ["pen"], 4096.0, A.mult)
    turn("3")

    def W(d, a, b):
        return T.ww[:, 96 * (5 - d) + a:96 * (5 - d) + b]

    for t in range(ROUNDS):
        last = t + 1 == ROUNDS
        q, s = codes[t]
        qk = ["q%d%d" % (t, i) for i in range(4)]
        for b in range(4):
            e = slice(128 * b, 128 * b + 128)
            mm(bank(T.psf, b, C), T.qe[:, e], T.se[:, e], q[:], s[:], qk + ["qe%d" % b], ["Bf%d" % b])
        cp(T.zz[:], T.xs[:].indirect(T.offg[:, 6 * t:6 * t + 6]), ["xs0", "xs1", "xs2", "xs3", "xsl", "xsr", "offg%d" % t], ["zz"])
        if t == 0:
            ts(T.offm[:], T.tab[:, 0:192:12], pc[11], A.add, tabs + ["pc11"], ["offm"], float(R0 + 41), A.add)
        tr(W(1, 0, 96), T.zz[:], ["zz"], ["w1"])
        win, ak = [T.a0, T.a1][t], "a%d" % t
        flags = ["ll%d" % d for d in range(1, 6)] + ["rr%d" % d for d in range(6)]
        fk = ["f0", "f1", "f2", "f3", "fz", "offp"]

        def numbered(kind, d):
            if kind == "f":
                act(T.fp[:, d:4 * C:4], bank(T.psf, d, C), ["Bf%d" % d], ["f%d" % d])
            elif kind == "g":
                e = slice(128 * d, 128 * d + 128)
                mm(bank(T.psf, d, 128), T.qe[:, e], T.se[:, e], q[:, 0:128], s[:, 0:128], qk, ["Bf%d" % d], False)
            elif kind == "w" and d == 5:
                tt(W(5, 27, 65), T.bw[:, 27:65], T.fw[:, 31:69], A.min, ["fw", "bw"], ["w5"])
            elif kind == "w":
                a, k = {2: (1, 1), 3: (2, 2), 4: (2, 2)}[d]
                tt(W(d, 32, 70 - d), W(a, 32, 70 - d), W(d - k, 32 + k, 70 - d + k), A.min, ["w%d" % a, "w%d" % (d - k)], ["w%d" % d])
            elif kind == "l":
                n, k = (37, 5) if d == 5 else (32, 1)
                tt(T.lr[:, 6 - d:6 * n:6], W(1, 32, 32 + n), W(k, 32 - d, 32 + n - d), A.is_lt, ["w1", "w%d" % k, "lr"], ["ll%d" % d])
            elif kind == "r":
                o = 1 if d == 5 else 0
                n = 37 - d if last else 32
                tt(T.lr[:, R0 + 6 + d - 6 * o:R0 + 6 + 6 * n:6], W(1, 32 - o, 32 + n), W(d, 33 - o, 33 + n), A.is_le,
                   ["w1", "w%d" % d, "lr"], ["rr%d" % d])
            elif t == 0 and d == 1:
                ts(T.eo[:, 3:515:4], T.jj[:], 1024.0, A.add, ["jj", "eo", "pc14"], ["eo"], pc[14], A.is_equal)
            elif t == 0:
                ts(T.offe[:, 0:1], T.pf[:, 9:10], 16.0, A.add, ["pf9"], ["offe"])

        def counts_out():
            if last:
                lin(T.oln[:], T.ln[:], 0.5, T.nb[:, 0:1], ["ln", "nb"], ["oln"])
                dma("y", T.ol[:, C:2 * C], T.oln[:], ["oln"], [])

        steps = {
            "fw": lambda: scan(T.fw[:, 27:72], T.rs[:, 0:45], W(1, 27, 72), 0.0, A.max, A.min, ["w1", "rs"], ["fw"]),
            "bw": lambda: scan(T.bw[:, 71:26:-1], T.rs[:, 0:45], T.ww[:, 455:410:-1], 0.0, A.max, A.min, ["w1", "rs"], ["bw"]),
            "gt": lambda: tt(T.gt[:, 0:5], T.ww[:, 32:417:96], T.ww[:, 421:32:-97], A.is_gt, ["w1", "w2", "w3", "w4", "w5"], ["gt"]),
            "ch": lambda: tt(T.ch[:], T.lr[:, R0 + 5:R0 + 197:6], T.lr[:, 31:222:6], A.max, ["rr5", "ll5"], ["ch"]),
            "hh": lambda: scan(T.hh[:, 6:198], T.lr[:, 0:192], T.lr[:, R0 + 6:R0 + 198], 0.0, A.mult, A.max, flags, ["hh"]),
            "ln": lambda: scan(T.ln[:], T.ch[:], T.ch[:], pc[4], A.add, A.add, ["ch", "pc4"], ["ln"]),
            "yy": lambda: scan(T.pd[:, 1:64:2], T.hh[:, 5:197:6], T.hh[:, 11:198:6], T.ln[:, 0:1], A.add, A.add,
                               ["hh", "hh0", "ln"], ["yy"]),
            "dl": lambda: scan(T.dl[:, 0:6], T.hh[:, 35:4:-6], T.gt[:, 0:6], 0.0, A.add, A.mult, ["hh", "hh0", "gt", "gt5"], ["dl"]),
            "or": lambda: tt(T.pm[:, 1:64:4], T.hh[:, 11:200:12], T.hh[:, 17:204:12], A.max, ["hh", "pm"], ["or"]),
            "ob": lambda: ts(T.offb[:, 0:1], T.ln[:, 31:32], 0.5, A.mult, ["ln", "pc9"], ["offb"], pc[9], A.add),
            "pl": lambda: scan(T.pl[:], T.pm[:], T.pd[:], 0.0, A.mult, A.add, ["or", "yy", "pm", "pm2", "pd0", "pd2"], ["pl"]),
            "bs": lambda: before(T.base[:, 0:1], T.j0[:], 2.0, pc[7], tabs + ["offb", "pc7"], ["base"]),
            "nb": lambda: before(T.nb[:, 0:1], T.j1[:], 1.0, pc[6], tabs + ["offb", "pc6"], ["nb"]),
            "of": lambda: ts(T.offs[:], T.pl[:, 2:64:4], T.base[:, 0:1], A.add, ["pl", "base", "dl"], ["offs"], T.dl[:, 5:6], A.subtract),
            "sc": lambda: cp(win[:].indirect(T.offs[:]), T.vc[:], ["offs", "vc"], [ak]),
            "n2": lambda: lin(T.n2[:], T.ln[:].indirect(T.offr[:]), 0.5, T.nb[:, 0:1], ["ln", "offr", "nb"], ["n2"]),
            "ol": counts_out,
            "e1": lambda: scan(T.e1[:], T.d0[:], win[:, 0:288], -4096.0, A.add, A.max, ["d0a", "d0b", ak], ["e1"]),
            "nt": lambda: tr(T.n2t[:], T.n2[:], ["n2"], ["n2t"]),
            "e2": lambda: scan(T.e2[:], T.pen[:], T.e1[:, 1:288:2], 0.0, A.add, A.min, ["pen", "e1"], ["e2"]),
            "on": lambda: ts(T.offn[:], T.n2t[:].indirect(T.offf[:]), float(CAP), A.min, ["n2t", "offf"], ["offn"]),
            "oa": lambda: ts(T.offa[:], T.n2t[:].indirect(T.offf[:, 0:1]), pc[15], A.max, ["n2t", "offf", "pc15"], ["offa"],
                             float(CAP), A.min),
            "oo": lambda: ts(T.offo[:], T.n2t[:].indirect(T.offe[:, 0:1]), float(CAP), A.min, ["n2t", "offe"], ["offo"]),
            "op": lambda: ts(T.offp[:], T.e2[:, 3:CAP:4], 1024.0, A.min, ["e2", "pc8"], ["offp"], pc[8], A.add),
            "pv": lambda: cp(T.pt[:, 0:16 * PV], T.fp[:, 0:4 * C + 4].indirect(T.offp[:, 0:PV]), fk, ["p0"]),
            "ps": lambda: act(T.pt[:, 16 * PV:576], T.fp[:, 0:4 * C + 4].indirect(T.offp[:, PV:36]), fk, ["p1"]),
        }
        for word in LISTS.split():
            if word in steps:
                steps[word]()
            else:
                numbered(word[0], int(word[1]))
        quant(T.qp[:], T.sp[:], T.pt[:], ["p0", "p1"], ["qp"])
        lq, lp = [(T.lq0, T.lp0), (T.lq1, T.lp1)][t]
        for b in (2, 0, 3, 1):
            e = slice(128 * b, 128 * b + 128)
            mm(bank(T.psr, b, CAP), lq[:, e], lp[:, e], T.qp[:], T.sp[:], ["qp", "lq%d" % t, "lp%d" % t], ["Br%d" % b])
        if last:
            lin(T.mg[:], T.lr[:].indirect(T.offm[:]), -1.0, 1.0, flags + ["offm", "lr"], ["mg"])
            quant(T.qv[:], T.sv[:], T.vt[:], ["vt"], ["qv"])
        else:
            for b in range(4):
                quant(T.qo[:, 128 * b:128 * b + 128], T.so[:, 128 * b:128 * b + 128], T.eo[:, 3 - b:515 - b], ["eo"], ["qo%d" % b])
            lin(T.a1[:, 0:288], T.tab[:, 0:288], 0.0, -2048.0, tabs, ["a1"])
            lin(T.md[:], T.tab[:, 0:256], 0.0, 1.0, tabs, ["md"])
        for b in (2, 0, 3, 1):
            if b < 2:
                ts(T.ht[:, b:4 * CAP:4], bank(T.psr, b, CAP), 0.03125, A.mult, ["Br%d" % b], ["h%d" % b])
            else:
                act(T.ht[:, b:4 * CAP:4], bank(T.psr, b, CAP), ["Br%d" % b], ["h%d" % b], 0.03125)
        if last:
            scan(T.mk[:], T.md[:], T.mg[:], 0.0, A.add, A.mult, ["mg", "md"], ["mk"])
            lin(T.olm[:], T.mk[:, 7:256:8], 1.0, pc[0], ["mk", "pc0"], ["olm"])
            dma("y", T.ol[:, 0:C], T.olm[:], ["olm"], [])
        else:
            act(T.md[:, 7:256:8], T.jj[:, 0:32], ["jj"], ["md"])
        quant(T.qh[:], T.sh[:], T.ht[:, 0:584], ["h0", "h1", "h2", "h3", "hz"], ["qh"])
        picked = {"A": (T["pa%d" % t], T["sa%d" % t], T.offa[:, 0:8], "offa"),
                  "B": (T["pb%d" % t], T["sb%d" % t], T.offo[:, 0:8], "offo")}

        new = tiles[t + 1]
        for word in PLAN[t].split():
            kind = word[0]
            if kind == "m":
                b = int(word[1])
                e = slice(128 * b, 128 * b + 128)
                mm(bank(T.psr, b, CAP), T.qe[:, e], T.se[:, e], T.qh[:, 0:CAP], T.sh[:, 0:CAP], ["qh", "qe%d" % b], ["Br%d" % b])
            elif kind == "P":
                pq, ps, off, ok = picked[word[1]]
                cp(pq[:].bitcast(dt.uint32), T.qh[:].bitcast(dt.uint32).indirect(off), ["qh", ok], [word])
            elif kind == "S":
                pq, ps, off, ok = picked[word[1]]
                if word[2] == "v":
                    cp(ps[:], T.sh[:].indirect(off), ["qh", ok], [word[:2]])
                else:
                    op("s", lambda: S.activation(ps[:], T.sh[:].indirect(off), ACT.Copy), ["qh", ok], [word[:2]])
            elif kind == "E":
                b = int(word[1])
                e = slice(128 * b, 128 * b + 128)

                def both():
                    out = bank(T.psf, b, 128)
                    g.tensor.matmul_mx(out, T.qe[:, e], T.se[:, e], picked["A"][0][:], picked["A"][1][:], False, False)
                    return g.tensor.matmul_mx(out, T.qo[:, e], T.so[:, e], picked["B"][0][:], picked["B"][1][:], False, True)

                op("p", both, ["PA", "PB", "SA", "SB", "qo%d" % b], ["Bf%d" % b], adds=True)
            elif kind == "k":
                b = int(word[1])
                (cp if word[2] == "v" else act)(new[:, b:512:4], bank(T.psf, b, 128), ["Bf%d" % b], ["T%d0" % b])
            elif kind == "q":
                quant_piece(t + 1, word[1:])
            elif kind == "t":
                turn(word[1:])
            elif kind == "o":
                k = int(word[1])
                dma(word[2], T.osc[4 * k:4 * k + 4, :], T.s2[32 * k:32 * k + 4, :], ["q20", "q21", "q22", "q23"], [])
            elif kind in "cyz":
                w = word[1:-1]
                a, z = span(w)
                if kind == "c":
                    dma(word[-1], T.oc[:, 4 * a:4 * z], T.q2[:, a:z].bitcast(dt.uint8), ["q2" + k for k in w], [])
                elif kind == "z":
                    dma(word[-1], T.y[:, a:z], T.ysb[:, a:z], ["y" + k for k in w], [])
                else:
                    (cp if word[-1] == "v" else act)(T.ysb[:, a:z], bank(T.psr, int(w[0]), z - a), ["Br" + w[0]], ["y" + k for k in w])
            elif kind == "h":
                b = int(word[1])
                (cp if word[2] == "v" else act)(T.dh[:, DW * b:DW * b + CAP], bank(T.psr, b, CAP), ["Br%d" % b], ["dh%d" % b])
            else:
                b, w = int(word[1]), word[2:]
                a, z = span(w)
                came = T.dh[:, DW * b:DW * b + CAP + 1].indirect(T.offn[:, a // 16:z // 16])
                got = T.gb[:, 512 * b + a:512 * b + z]
                out = new[:, 4 * a + b:4 * z:4]
                gk, tk = ["g%d%s" % (b, k) for k in w], ["T%d%s" % (b, k) for k in w]
                if kind == "f":
                    act(got, came, ["dh%d" % b, "dz", "offn"], gk)
                elif kind == "d":
                    tt(out, came, T.fp[:, 4 * a + b:4 * z:4], A.add, ["dh%d" % b, "dz", "offn", "f%d" % b], tk)
                else:
                    tt(out, bank(T.psf, b, z - a, a), got, A.add, ["Bf%d" % b] + gk, tk)

    g.wait_ge(T.sem.sent, sent[0])
    for sem, val in count.items():
        if waited.get(sem, 0) < val:
            g.wait_ge(T.sem[sem], val)
